import numpy as np
import ml_dtypes


def mxq(x, axis, fmt="e4m3"):
    dtype, down = {"e4m3": (ml_dtypes.float8_e4m3fn, 7), "e5m2": (ml_dtypes.float8_e5m2, 14)}[fmt]
    v = np.moveaxis(np.asarray(x, np.float32).astype(ml_dtypes.bfloat16).astype(np.float64), axis, -1)
    blocks = v.reshape(v.shape[:-1] + (-1, 32))
    amax = np.abs(blocks).max(-1, keepdims=True)
    byte = np.maximum(np.where(amax > 0, np.frexp(amax)[1] - 1 + 127, 0) - down, 1)
    scale = np.exp2(byte - 127.0)
    codes = (blocks / scale).astype(np.float32).astype(dtype).astype(np.float64)
    return np.moveaxis((codes * scale).reshape(v.shape), -1, axis)


WIDE = False


def mx_kscale(k):
    if not WIDE:
        return np.ones(k)
    levels = np.array([10, -10, 5, -5, 0])
    if k % 512:
        return np.exp2(np.random.permutation(np.resize(levels, k // 32))).repeat(32)
    a = np.empty((k // 512, 16))
    for p in range(k // 512):
        a[p, :8] = np.random.permutation(np.resize(levels, 8))
        for g in range(8):
            far = levels[np.abs(levels - a[p, g]) >= 10]
            a[p, g + 8] = far[np.random.randint(len(far))]
    return np.exp2(a.ravel()).repeat(32)


def f64(x):
    return np.asarray(x).astype(np.float64)


def striped(idx):
    return np.tile(idx.reshape(-1, 16).T, (8, 1)).astype(np.uint16)


def unstriped(offs):
    return offs[:16].T.reshape(-1).astype(np.int64)


def striped8(idx):
    return np.concatenate([x.reshape(-1, 16).T for x in idx]).astype(np.uint16)


def runs(offs, k):
    lists = np.stack([offs[16 * r : 16 * r + 16].T.reshape(-1) for r in range(8)]).astype(np.int64)
    return lists[np.arange(k) % 512 // 64]


def pack_weight(w):
    k, n = w.shape
    w = f64(np.asarray(w, np.float32).astype(ml_dtypes.bfloat16)).reshape(k // 32, 32, n)
    amax = np.abs(w).max(1)
    byte = np.clip(np.where(amax > 0, np.frexp(amax)[1] - 1 + 127 - 7, 1), 1, 254)
    scaled = (w * np.exp2(127.0 - byte)[:, None, :]).reshape(k, n).astype(np.float32)
    words = np.ascontiguousarray(scaled.reshape(k // 512, 128, 4, n).transpose(0, 1, 3, 2)).astype(ml_dtypes.float8_e4m3fn).view(np.uint8)
    return words, np.ascontiguousarray(byte.astype(np.uint8).reshape(k // 512, 16, n))


def unpack_weight(words, scales):
    g, p, n, _ = words.shape
    vals = np.ascontiguousarray(words).view(ml_dtypes.float8_e4m3fn).astype(np.float64) * np.repeat(np.exp2(scales.astype(np.float64) - 127.0), 8, axis=1)[..., None]
    return vals.transpose(0, 1, 3, 2).reshape(g * 512, n)

def planes(y):
    n, m = y.shape
    v = y.astype(np.float32).astype(ml_dtypes.bfloat16).astype(np.float64).reshape(n // 32, 32, m)
    top = np.abs(v).max(1)
    byte = np.clip(np.where(top > 0, np.frexp(top)[1] - 1 + 127 - 7, 1), 1, 254)
    codes = (v * np.exp2(127.0 - byte)[:, None, :]).reshape(n, m).astype(np.float32).astype(ml_dtypes.float8_e4m3fn).view(np.uint8)
    words = codes.reshape(n // 512, 128, 4, m).transpose(0, 1, 3, 2)
    return np.ascontiguousarray(words), np.ascontiguousarray(byte.astype(np.uint8).reshape(n // 512, 16, m))


K, T, S, V, H, W = 512, 2048, 512, 512, 512, 2048


def setup_inputs():
    n = np.random.standard_normal
    s = mx_kscale(K)[:, None]
    u = mx_kscale(S)
    packed_xT = pack_weight(n((K, T)) * s)
    packed_w1 = pack_weight(n((K, H)) / np.sqrt(K) / s)
    packed_w2 = pack_weight(n((K, H)) / np.sqrt(K) / s)
    return {
        "x_words": packed_xT[0],
        "x_scales": packed_xT[1],
        "w1_words": packed_w1[0],
        "w1_scales": packed_w1[1],
        "w2_words": packed_w2[0],
        "w2_scales": packed_w2[1],
        "ga": (np.random.uniform(0.5, 1.5, (H, 1)) * u[:, None]).astype(np.float32),
        "gb": (np.random.uniform(0.5, 1.5, (H, 1)) / u[:, None]).astype(np.float32),
        "offs": striped(np.random.permutation(T)[:S]),
        "two": striped(np.random.permutation(T)[:V]),
        "n1": striped(np.random.randint(0, S, W)),
        "n2": striped8(np.stack([np.random.permutation(V) for _ in range(8)])),
        "n3": striped8(np.stack([np.random.permutation(V) for _ in range(8)])),
        "n4": striped(np.random.permutation(V)),
        "n5": striped(np.random.permutation(V)),
    }


def reference(x_words, x_scales, w1_words, w1_scales, w2_words, w2_scales, ga, gb, offs, two, n1, n2, n3, n4, n5):
    xq = unpack_weight(x_words, x_scales)[:, unstriped(offs)]
    a = unpack_weight(w1_words, w1_scales).T @ xq
    mb = a[:, unstriped(n1)]
    sq = (mb) ** 2
    qs = sq.reshape(H, S, 4).sum(axis=2)
    z = f64(ga) * (a / np.sqrt(qs + 0.5))
    x_two = unpack_weight(x_words, x_scales)[:, unstriped(two)]
    b = unpack_weight(w2_words, w2_scales).T @ x_two
    z2 = f64(gb) * ((b[np.arange(H)[:, None], runs(n2, H)]) / (np.abs(b) + np.abs(b[np.arange(H)[:, None], runs(n3, H)]) + 0.5))
    s = 0.0625 * ((mxq(z, 0, "e4m3").T @ mxq(z2, 0, "e4m3")))
    st = s + s[:, unstriped(n4)]
    out_0 = st * (np.tanh(st[:, unstriped(n5)]))
    return (out_0,) + planes(out_0)

@@ -1,0 +1,256 @@
+from contextlib import ExitStack
+
+import concourse.mybir as mybir
+from concourse.masks import make_identity
+
+F32 = mybir.dt.float32
+BF16 = mybir.dt.bfloat16
+I32 = mybir.dt.int32
+U32 = mybir.dt.uint32
+U16 = mybir.dt.uint16
+U8 = mybir.dt.uint8
+FP8X4 = mybir.dt.float8_e4m3fn_x4
+ALU = mybir.AluOpType
+ACT = mybir.ActivationFunctionType
+
+P = 128
+PACK = 4
+N = 512
+T = 2048
+HALF = N // 2
+LIST_COL = 16
+SPARE = 16
+
+FLOPS = 3 * 2 * N * N * N
+
+
+def tile_picked_kqgvarnorm2hopp_none_po_kernel(
+    tc, x_words, x_scales, w1_words, w1_scales, w2_words, w2_scales, ga, gb,
+    offs, two, n1, n2, n3, n4, n5, out_0, out_1, out_2,
+):
+    nc = tc.nc
+    with ExitStack() as ctx:
+        keep = ctx.enter_context(tc.tile_pool(name="keep", bufs=1))
+        ring = ctx.enter_context(tc.tile_pool(name="ring", bufs=4))
+        members = ctx.enter_context(tc.tile_pool(name="members", bufs=6))
+        mm_ps = ctx.enter_context(tc.psum_pool(name="mm_ps", bufs=3))
+        sum_ps = ctx.enter_context(tc.psum_pool(name="sum_ps", bufs=3))
+        back_ps = ctx.enter_context(tc.psum_pool(name="back_ps", bufs=2))
+
+        def load_list(src, name):
+            tile = keep.tile(list(src.shape), U16, name=name)
+            nc.sync.dma_start(tile[:], src)
+            return tile
+
+        def load_words(src, name):
+            tile = keep.tile([P, src.shape[2]], I32, name=name, align_bytes=64)
+            nc.sync.dma_start(tile[:], src[0].rearrange("p c r -> p (c r)").bitcast(I32))
+            return tile
+
+        def load_scales(src, name, clear, queue):
+            tile = keep.tile([P, src.shape[2]], U8, name=name, align_bytes=64)
+            clear.memset(tile[:].bitcast(I32), 0)
+            for q in range(4):
+                queue.dma_start(tile[32 * q : 32 * q + 4, :].bitcast(I32), src[0, 4 * q : 4 * q + 4, :].bitcast(I32))
+            return tile
+
+        def entries(lst, first, count):
+            return lst[:, first // LIST_COL : (first + count) // LIST_COL]
+
+        xw = load_words(x_words, "xw")
+        xs = load_scales(x_scales, "xs", nc.vector, nc.sync)
+        offs_t = load_list(offs, "offs_t")
+        w1w = load_words(w1_words, "w1w")
+        two_t = load_list(two, "two_t")
+        w1s = load_scales(w1_scales, "w1s", nc.gpsimd, nc.gpsimd)
+        ident = keep.tile([P, P], F32, name="ident")
+        make_identity(nc, ident[:])
+        n1_t = load_list(n1, "n1_t")
+        w2w = load_words(w2_words, "w2w")
+        w2s = load_scales(w2_scales, "w2s", nc.vector, nc.sync)
+        n3_t = load_list(n3, "n3_t")
+        n2_t = load_list(n2, "n2_t")
+        ga_t = keep.tile([P, PACK], F32, name="ga_t")
+        nc.sync.dma_start(ga_t[:], ga.rearrange("(p t) o -> p (t o)", t=PACK))
+        gb_t = keep.tile([P, PACK], F32, name="gb_t")
+        nc.sync.dma_start(gb_t[:], gb.rearrange("(p t) o -> p (t o)", t=PACK))
+        n4_t = load_list(n4, "n4_t")
+        n5_t = load_list(n5, "n5_t")
+
+        half = keep.tile([P, 1], F32, name="half")
+        nc.vector.memset(half[:], 0.5)
+        sq = [keep.tile([P, N + SPARE], F32, name="sq%d" % t) for t in range(PACK)]
+        for t in range(PACK):
+            nc.vector.memset(sq[t][:, N:], 0.0)
+
+        def pick_scales(lst, name):
+            tile = keep.tile([P, N], U8, name=name, align_bytes=64)
+            nc.vector.tensor_copy(tile[:], xs[:].indirect(lst[:]))
+            return tile
+
+        def pick_words(lst, name):
+            tile = keep.tile([P, N], U32, name=name, align_bytes=64)
+            nc.vector.tensor_copy(tile[:], xw[:].bitcast(U32).indirect(lst[:]))
+            return tile
+
+        def deal(src, dtype, name):
+            tile = keep.tile([P, N], dtype, name=name, align_bytes=64)
+            nc.vector.tensor_copy(
+                tile[:].rearrange("p (t m) -> p t m", t=PACK), src[:].rearrange("p (m t) -> p t m", t=PACK)
+            )
+            return tile
+
+        def product(lhs_words, lhs_scales, rhs_words, rhs_scales, t):
+            acc = mm_ps.tile([P, N], F32, name="acc")
+            cols = slice(t * P, (t + 1) * P)
+            nc.tensor.matmul_mx(
+                out=acc[:], lhsT=lhs_words[:, cols].bitcast(FP8X4), lhsT_scale=lhs_scales[:, cols],
+                rhs=rhs_words[:].bitcast(FP8X4), rhs_scale=rhs_scales[:], start=True, stop=True,
+            )
+            return acc
+
+        xa_s = pick_scales(offs_t, "xa_s")
+        w1w_d = deal(w1w, I32, "w1w_d")
+        xb_s = pick_scales(two_t, "xb_s")
+        xa_w = pick_words(offs_t, "xa_w")
+        w1s_d = deal(w1s, U8, "w1s_d")
+
+        a_sb = []
+        for t in range(PACK):
+            acc = product(w1w_d, w1s_d, xa_w, xa_s, t)
+            a_t = keep.tile([P, N], F32, name="a%d" % t)
+            if t == 0:
+                nc.scalar.activation(sq[t][:, :N], acc[:], ACT.Square)
+                nc.vector.tensor_copy(a_t[:], acc[:])
+            else:
+                nc.vector.tensor_copy(a_t[:], acc[:])
+                nc.vector.tensor_tensor(sq[t][:, :N], acc[:], a_t[:], ALU.mult)
+            a_sb.append(a_t)
+
+        sums = {}
+
+        def member_sums(c, t):
+            if c not in sums:
+                sums[c] = sum_ps.tile([P, PACK, P], F32, name="sums")
+            mb = members.tile([P, N], F32, name="mb")
+            nc.scalar.activation(mb[:], sq[t][:].indirect(entries(n1_t, c * N, N)), ACT.Copy)
+            for e in range(4):
+                nc.tensor.matmul(
+                    sums[c][:, t, :], lhsT=mb[:, e:N:4], rhs=ident[:], is_transpose=True, start=(e == 0), stop=(e == 3)
+                )
+
+        z_il = keep.tile([P, PACK, P, PACK], BF16, name="z_il", align_bytes=64)
+
+        def finish_z(c):
+            r_t = ring.tile([P, PACK, P], F32, name="r_t")
+            nc.scalar.activation(
+                r_t[:].rearrange("p t m -> p (t m)"), sums[c][:].rearrange("p t m -> p (t m)"),
+                ACT.Abs_reciprocal_sqrt, bias=half[:],
+            )
+            r_ps = back_ps.tile([P, PACK, P], F32, name="r_ps")
+            for t in range(PACK):
+                nc.tensor.transpose(r_ps[:, t, :], r_t[:, t, :], ident[:])
+            z_c = ring.tile([P, PACK, P], BF16, name="z_c")
+            for t in range(PACK):
+                nc.vector.scalar_tensor_tensor(
+                    z_c[:, t, :], r_ps[:, t, :], ga_t[:, t : t + 1], a_sb[t][:, c * P : (c + 1) * P], ALU.mult, ALU.mult
+                )
+            nc.vector.tensor_copy(
+                z_il[:, :, 32 * c : 32 * (c + 1), :], z_c[:].rearrange("p k (m u) -> p u m k", u=PACK)
+            )
+
+        for t in range(PACK):
+            member_sums(0, t)
+            member_sums(1, t)
+
+        xb_w = pick_words(two_t, "xb_w")
+        w2w_d = deal(w2w, I32, "w2w_d")
+        w2s_d = deal(w2s, U8, "w2s_d")
+        b_sb, b_abs = [], []
+        for t in range(PACK):
+            acc = product(w2w_d, w2s_d, xb_w, xb_s, t)
+            b_t = keep.tile([P, N], F32, name="b%d" % t)
+            nc.vector.tensor_copy(b_t[:], acc[:])
+            abs_t = keep.tile([P, N], F32, name="babs%d" % t)
+            nc.vector.scalar_tensor_tensor(abs_t[:], acc[:], -1.0, b_t[:], ALU.mult, ALU.max)
+            b_sb.append(b_t)
+            b_abs.append(abs_t)
+
+        z2_t = keep.tile([P, PACK, N], BF16, name="z2_t")
+        roots = []
+        for t in range(PACK):
+            g3 = ring.tile([P, N], F32, name="g3")
+            for h in range(2):
+                nc.scalar.activation(
+                    g3[:, h * HALF : (h + 1) * HALF], b_abs[t][:].indirect(entries(n3_t, h * HALF, HALF)), ACT.Copy
+                )
+            den = ring.tile([P, N], F32, name="den")
+            nc.vector.tensor_tensor(den[:], g3[:], b_abs[t][:], ALU.add)
+            root = keep.tile([P, N], F32, name="root%d" % t)
+            nc.scalar.activation(root[:], den[:], ACT.Abs_reciprocal_sqrt, bias=half[:])
+            roots.append(root)
+        finish_z(0)
+        finish_z(1)
+        for t in range(PACK):
+            member_sums(2, t)
+        for t in range(PACK):
+            u = ring.tile([P, N], F32, name="u")
+            for h in range(2):
+                cols = slice(h * HALF, (h + 1) * HALF)
+                nc.vector.tensor_tensor(
+                    u[:, cols], b_sb[t][:].indirect(entries(n2_t, h * HALF, HALF)), roots[t][:, cols], ALU.mult
+                )
+            nc.vector.scalar_tensor_tensor(z2_t[:, t, :], u[:], gb_t[:, t : t + 1], roots[t][:], ALU.mult, ALU.mult)
+        z2_il = keep.tile([P, N, PACK], BF16, name="z2_il", align_bytes=64)
+        nc.vector.tensor_copy(z2_il[:], z2_t[:].rearrange("p k v -> p v k"))
+        z2_w = keep.tile([P, N], U32, name="z2_w", align_bytes=64)
+        z2_s = keep.tile([P, N], U8, name="z2_s", align_bytes=64)
+        nc.vector.quantize_mx(out=z2_w[:].bitcast(FP8X4), scales=z2_s[:], in_=z2_il[:].rearrange("p v k -> p (v k)"))
+
+        member_sums(3, 0)
+        finish_z(2)
+        for t in range(1, PACK):
+            member_sums(3, t)
+        finish_z(3)
+
+        z_w = keep.tile([P, N], U32, name="z_w", align_bytes=64)
+        z_s = keep.tile([P, N], U8, name="z_s", align_bytes=64)
+        for t in range(PACK):
+            cols = slice(t * P, (t + 1) * P)
+            nc.vector.quantize_mx(
+                out=z_w[:, cols].bitcast(FP8X4), scales=z_s[:, cols], in_=z_il[:, t].rearrange("p m k -> p (m k)")
+            )
+
+        y = keep.tile([P, PACK, N], F32, name="y")
+        out_rows = out_0.rearrange("(p t) v -> p t v", t=PACK)
+        for t in range(PACK):
+            acc = product(z_w, z_s, z2_w, z2_s, t)
+            s2 = ring.tile([P, N], F32, name="s2")
+            nc.scalar.activation(s2[:], acc[:], ACT.Copy, scale=0.125)
+            g4 = ring.tile([P, N], F32, name="g4")
+            for h in range(2):
+                cols = slice(h * HALF, (h + 1) * HALF)
+                looked_up = s2[:].indirect(entries(n4_t, h * HALF, HALF))
+                if t == 1:
+                    nc.scalar.activation(g4[:, cols], looked_up, ACT.Copy)
+                else:
+                    nc.vector.tensor_copy(g4[:, cols], looked_up)
+            st2 = ring.tile([P, N], F32, name="st2")
+            nc.vector.scalar_tensor_tensor(st2[:], acc[:], 0.125, g4[:], ALU.mult, ALU.add)
+            sg = ring.tile([P, N], F32, name="sg")
+            for h in range(2):
+                nc.scalar.activation(
+                    sg[:, h * HALF : (h + 1) * HALF], st2[:].indirect(entries(n5_t, h * HALF, HALF)), ACT.Sigmoid
+                )
+            nc.vector.scalar_tensor_tensor(y[:, t, :], sg[:], -0.5, st2[:], ALU.add, ALU.mult)
+            nc.sync.dma_start(out_rows[:, t, :], y[:, t, :])
+
+        y_il = keep.tile([P, N, PACK], BF16, name="y_il", align_bytes=64)
+        nc.vector.tensor_copy(y_il[:], y[:].rearrange("p t v -> p v t"))
+        y_w = keep.tile([P, N], I32, name="y_w", align_bytes=64)
+        y_s = keep.tile([P, N], U8, name="y_s", align_bytes=64)
+        nc.vector.quantize_mx(out=y_w[:].bitcast(FP8X4), scales=y_s[:], in_=y_il[:].rearrange("p v t -> p (v t)"))
+        nc.sync.dma_start(out_1[0].rearrange("p c r -> p (c r)").bitcast(I32), y_w[:])
+        for q in range(4):
+            queue = nc.sync if q < 2 else nc.scalar
+            queue.dma_start(out_2[0, 4 * q : 4 * q + 4, :].bitcast(I32), y_s[32 * q : 32 * q + 4, :].bitcast(I32))

@@ -31,51 +31,60 @@ def tile_picked_kqgvarnorm2hopp_none_po_kernel(
     nc = tc.nc
     with ExitStack() as ctx:
         keep = ctx.enter_context(tc.tile_pool(name="keep", bufs=1))
-        ring = ctx.enter_context(tc.tile_pool(name="ring", bufs=4))
-        members = ctx.enter_context(tc.tile_pool(name="members", bufs=6))
-        mm_ps = ctx.enter_context(tc.psum_pool(name="mm_ps", bufs=3))
-        sum_ps = ctx.enter_context(tc.psum_pool(name="sum_ps", bufs=3))
-        back_ps = ctx.enter_context(tc.psum_pool(name="back_ps", bufs=2))
+        psum = ctx.enter_context(tc.psum_pool(name="psum", bufs=1))
+        bank = [psum.tile([P, N], F32, name="bank%d" % i) for i in range(8)]
 
         def load_list(src, name):
             tile = keep.tile(list(src.shape), U16, name=name)
             nc.sync.dma_start(tile[:], src)
             return tile
 
-        def load_words(src, name):
-            tile = keep.tile([P, src.shape[2]], I32, name=name, align_bytes=64)
+        def load_words(tile, src):
             nc.sync.dma_start(tile[:], src[0].rearrange("p c r -> p (c r)").bitcast(I32))
+
+        def scale_tile(width, name, clear):
+            tile = keep.tile([P, width], U8, name=name, align_bytes=64)
+            clear.memset(tile[:].bitcast(I32), 0)
             return tile
 
-        def load_scales(src, name, clear, queue):
-            tile = keep.tile([P, src.shape[2]], U8, name=name, align_bytes=64)
-            clear.memset(tile[:].bitcast(I32), 0)
+        def load_scales(tile, src, queues):
             for q in range(4):
-                queue.dma_start(tile[32 * q : 32 * q + 4, :].bitcast(I32), src[0, 4 * q : 4 * q + 4, :].bitcast(I32))
-            return tile
+                queues[q].dma_start(
+                    tile[32 * q : 32 * q + 4, :].bitcast(I32), src[0, 4 * q : 4 * q + 4, :].bitcast(I32)
+                )
 
         def entries(lst, first, count):
             return lst[:, first // LIST_COL : (first + count) // LIST_COL]
 
-        xw = load_words(x_words, "xw")
-        xs = load_scales(x_scales, "xs", nc.vector, nc.sync)
+        w1s = scale_tile(N, "w1s", nc.gpsimd)
+        xs = scale_tile(T, "xs", nc.vector)
+        w2s = scale_tile(N, "w2s", nc.vector)
         offs_t = load_list(offs, "offs_t")
-        w1w = load_words(w1_words, "w1w")
+        xs_raw = keep.tile([P, T], U8, name="xs_raw", align_bytes=64)
+        load_scales(xs_raw, x_scales, [nc.sync] * 4)
+        xw = keep.tile([P, T], I32, name="xw", align_bytes=64)
+        load_words(xw, x_words)
+        w1w = keep.tile([P, N], I32, name="w1w", align_bytes=64)
+        load_words(w1w, w1_words)
+        load_scales(w1s, w1_scales, [nc.sync] * 4)
         two_t = load_list(two, "two_t")
-        w1s = load_scales(w1_scales, "w1s", nc.gpsimd, nc.gpsimd)
-        ident = keep.tile([P, P], F32, name="ident")
-        make_identity(nc, ident[:])
         n1_t = load_list(n1, "n1_t")
-        w2w = load_words(w2_words, "w2w")
-        w2s = load_scales(w2_scales, "w2s", nc.vector, nc.sync)
+        w2w = keep.tile([P, N], I32, name="w2w", align_bytes=64)
+        load_words(w2w, w2_words)
+        load_scales(w2s, w2_scales, [nc.sync] * 4)
         n3_t = load_list(n3, "n3_t")
         n2_t = load_list(n2, "n2_t")
-        ga_t = keep.tile([P, PACK], F32, name="ga_t")
-        nc.sync.dma_start(ga_t[:], ga.rearrange("(p t) o -> p (t o)", t=PACK))
-        gb_t = keep.tile([P, PACK], F32, name="gb_t")
-        nc.sync.dma_start(gb_t[:], gb.rearrange("(p t) o -> p (t o)", t=PACK))
         n4_t = load_list(n4, "n4_t")
         n5_t = load_list(n5, "n5_t")
+        ident = keep.tile([P, P], F32, name="ident")
+        make_identity(nc, ident[:])
+        ga_t = keep.tile([P, PACK], F32, name="ga_t")
+        nc.gpsimd.dma_start(ga_t[:], ga.rearrange("(p t) o -> p (t o)", t=PACK))
+        gb_t = keep.tile([P, PACK], F32, name="gb_t")
+        nc.gpsimd.dma_start(gb_t[:], gb.rearrange("(p t) o -> p (t o)", t=PACK))
+        for q in range(4):
+            live = slice(32 * q, 32 * q + 4)
+            nc.vector.tensor_copy(xs[live, :].bitcast(I32), xs_raw[live, :].bitcast(I32))
 
         half = keep.tile([P, 1], F32, name="half")
         nc.vector.memset(half[:], 0.5)
@@ -93,125 +102,207 @@ def tile_picked_kqgvarnorm2hopp_none_po_kernel(
             nc.vector.tensor_copy(tile[:], xw[:].bitcast(U32).indirect(lst[:]))
             return tile
 
-        def deal(src, dtype, name):
-            tile = keep.tile([P, N], dtype, name=name, align_bytes=64)
-            nc.vector.tensor_copy(
-                tile[:].rearrange("p (t m) -> p t m", t=PACK), src[:].rearrange("p (m t) -> p t m", t=PACK)
+        def deal(dealt, src, first, last, engine=nc.vector):
+            engine.tensor_copy(
+                dealt[:].rearrange("p (t m) -> p t m", t=PACK)[:, first:last, :],
+                src[:].rearrange("p (m t) -> p t m", t=PACK)[:, first:last, :],
             )
-            return tile
 
-        def product(lhs_words, lhs_scales, rhs_words, rhs_scales, t):
-            acc = mm_ps.tile([P, N], F32, name="acc")
+        whole, left, right = slice(0, N), slice(0, HALF), slice(HALF, N)
+
+        def product(acc, lhs_words, lhs_scales, rhs_words, rhs_scales, t):
             cols = slice(t * P, (t + 1) * P)
             nc.tensor.matmul_mx(
                 out=acc[:], lhsT=lhs_words[:, cols].bitcast(FP8X4), lhsT_scale=lhs_scales[:, cols],
                 rhs=rhs_words[:].bitcast(FP8X4), rhs_scale=rhs_scales[:], start=True, stop=True,
             )
-            return acc
+
+        def rows(name):
+            return [keep.tile([P, N], F32, name="%s%d" % (name, t)) for t in range(PACK)]
 
         xa_s = pick_scales(offs_t, "xa_s")
-        w1w_d = deal(w1w, I32, "w1w_d")
-        xb_s = pick_scales(two_t, "xb_s")
         xa_w = pick_words(offs_t, "xa_w")
-        w1s_d = deal(w1s, U8, "w1s_d")
+        w1w_d = keep.tile([P, N], I32, name="w1w_d", align_bytes=64)
+        w1s_d = keep.tile([P, N], U8, name="w1s_d", align_bytes=64)
+        a_bank = bank[0:4]
+        deal(w1w_d, w1w, 0, 1)
+        deal(w1s_d, w1s, 0, 1)
+        product(a_bank[0], w1w_d, w1s_d, xa_w, xa_s, 0)
+        nc.scalar.activation(sq[0][:, :N], a_bank[0][:], ACT.Square)
+        deal(w1w_d, w1w, 1, PACK)
+        deal(w1s_d, w1s, 1, PACK)
+        for t in range(1, PACK):
+            product(a_bank[t], w1w_d, w1s_d, xa_w, xa_s, t)
+        xb_s = pick_scales(two_t, "xb_s")
 
-        a_sb = []
-        for t in range(PACK):
-            acc = product(w1w_d, w1s_d, xa_w, xa_s, t)
-            a_t = keep.tile([P, N], F32, name="a%d" % t)
-            if t == 0:
-                nc.scalar.activation(sq[t][:, :N], acc[:], ACT.Square)
-                nc.vector.tensor_copy(a_t[:], acc[:])
-            else:
-                nc.vector.tensor_copy(a_t[:], acc[:])
-                nc.vector.tensor_tensor(sq[t][:, :N], acc[:], a_t[:], ALU.mult)
-            a_sb.append(a_t)
+        a_sb, b_sb, b_abs, g3, den, root, mb, r_t = (rows(n) for n in ("a", "b", "babs", "g3_", "den", "root", "mb", "rt"))
+        g3 = [g3[0], g3[1], den[0], den[1]]
+        b_bank = [bank[6], bank[7], bank[1], bank[2]]
+        sum_bank = [bank[4], bank[5], bank[6], bank[7]]
+        back_bank = [bank[3], bank[0], bank[4], bank[5]]
+        s_bank = [bank[0], bank[3], bank[6], bank[4]]
 
-        sums = {}
-
-        def member_sums(c, t):
-            if c not in sums:
-                sums[c] = sum_ps.tile([P, PACK, P], F32, name="sums")
-            mb = members.tile([P, N], F32, name="mb")
-            nc.scalar.activation(mb[:], sq[t][:].indirect(entries(n1_t, c * N, N)), ACT.Copy)
+        def member_sums(c, t, buf):
+            nc.scalar.activation(buf[:], sq[t][:].indirect(entries(n1_t, c * N, N)), ACT.Copy)
             for e in range(4):
                 nc.tensor.matmul(
-                    sums[c][:, t, :], lhsT=mb[:, e:N:4], rhs=ident[:], is_transpose=True, start=(e == 0), stop=(e == 3)
+                    sum_bank[c][:, t * P : (t + 1) * P], lhsT=buf[:, e:N:4], rhs=ident[:], is_transpose=True,
+                    start=(e == 0), stop=(e == 3),
                 )
 
+        z_c = [keep.tile([P, PACK, P], BF16, name="z_c%d" % i) for i in range(2)]
         z_il = keep.tile([P, PACK, P, PACK], BF16, name="z_il", align_bytes=64)
 
-        def finish_z(c):
-            r_t = ring.tile([P, PACK, P], F32, name="r_t")
-            nc.scalar.activation(
-                r_t[:].rearrange("p t m -> p (t m)"), sums[c][:].rearrange("p t m -> p (t m)"),
-                ACT.Abs_reciprocal_sqrt, bias=half[:],
-            )
-            r_ps = back_ps.tile([P, PACK, P], F32, name="r_ps")
-            for t in range(PACK):
-                nc.tensor.transpose(r_ps[:, t, :], r_t[:, t, :], ident[:])
-            z_c = ring.tile([P, PACK, P], BF16, name="z_c")
-            for t in range(PACK):
+        def roots_of_sums(c, buf, tiles=range(PACK)):
+            cols = slice(tiles[0] * P, (tiles[-1] + 1) * P)
+            nc.scalar.activation(buf[:, cols], sum_bank[c][:, cols], ACT.Abs_reciprocal_sqrt, bias=half[:])
+            for t in tiles:
+                nc.tensor.transpose(back_bank[c][:, t * P : (t + 1) * P], buf[:, t * P : (t + 1) * P], ident[:])
+
+        def z_chunk(c, tiles=range(PACK)):
+            for t in tiles:
                 nc.vector.scalar_tensor_tensor(
-                    z_c[:, t, :], r_ps[:, t, :], ga_t[:, t : t + 1], a_sb[t][:, c * P : (c + 1) * P], ALU.mult, ALU.mult
+                    z_c[c % 2][:, t, :], back_bank[c][:, t * P : (t + 1) * P], ga_t[:, t : t + 1],
+                    a_sb[t][:, c * P : (c + 1) * P], ALU.mult, ALU.mult,
                 )
+
+        def z_weave(c, tiles=PACK):
             nc.vector.tensor_copy(
-                z_il[:, :, 32 * c : 32 * (c + 1), :], z_c[:].rearrange("p k (m u) -> p u m k", u=PACK)
+                z_il[:, :, 32 * c : 32 * (c + 1), :tiles],
+                z_c[c % 2][:, :tiles, :].rearrange("p k (m u) -> p u m k", u=PACK),
             )
 
-        for t in range(PACK):
-            member_sums(0, t)
-            member_sums(1, t)
+        def b_out(t):
+            nc.vector.tensor_copy(b_sb[t][:], b_bank[t][:])
+            nc.vector.scalar_tensor_tensor(b_abs[t][:], b_bank[t][:], -1.0, b_sb[t][:], ALU.mult, ALU.max)
 
-        xb_w = pick_words(two_t, "xb_w")
-        w2w_d = deal(w2w, I32, "w2w_d")
-        w2s_d = deal(w2s, U8, "w2s_d")
-        b_sb, b_abs = [], []
-        for t in range(PACK):
-            acc = product(w2w_d, w2s_d, xb_w, xb_s, t)
-            b_t = keep.tile([P, N], F32, name="b%d" % t)
-            nc.vector.tensor_copy(b_t[:], acc[:])
-            abs_t = keep.tile([P, N], F32, name="babs%d" % t)
-            nc.vector.scalar_tensor_tensor(abs_t[:], acc[:], -1.0, b_t[:], ALU.mult, ALU.max)
-            b_sb.append(b_t)
-            b_abs.append(abs_t)
-
-        z2_t = keep.tile([P, PACK, N], BF16, name="z2_t")
-        roots = []
-        for t in range(PACK):
-            g3 = ring.tile([P, N], F32, name="g3")
+        def fetch_n3(t):
             for h in range(2):
                 nc.scalar.activation(
-                    g3[:, h * HALF : (h + 1) * HALF], b_abs[t][:].indirect(entries(n3_t, h * HALF, HALF)), ACT.Copy
+                    g3[t][:, h * HALF : (h + 1) * HALF], b_abs[t][:].indirect(entries(n3_t, h * HALF, HALF)), ACT.Copy
                 )
-            den = ring.tile([P, N], F32, name="den")
-            nc.vector.tensor_tensor(den[:], g3[:], b_abs[t][:], ALU.add)
-            root = keep.tile([P, N], F32, name="root%d" % t)
-            nc.scalar.activation(root[:], den[:], ACT.Abs_reciprocal_sqrt, bias=half[:])
-            roots.append(root)
-        finish_z(0)
-        finish_z(1)
-        for t in range(PACK):
-            member_sums(2, t)
-        for t in range(PACK):
-            u = ring.tile([P, N], F32, name="u")
+
+        def den_sum(t):
+            nc.vector.tensor_tensor(den[t][:], g3[t][:], b_abs[t][:], ALU.add)
+
+        def den_root(t):
+            nc.scalar.activation(root[t][:], den[t][:], ACT.Abs_reciprocal_sqrt, bias=half[:])
+
+        u = rows("u")
+        z2_t = keep.tile([P, PACK, N], BF16, name="z2_t")
+
+        def fetch_n2(t):
             for h in range(2):
                 cols = slice(h * HALF, (h + 1) * HALF)
                 nc.vector.tensor_tensor(
-                    u[:, cols], b_sb[t][:].indirect(entries(n2_t, h * HALF, HALF)), roots[t][:, cols], ALU.mult
+                    u[t][:, cols], b_sb[t][:].indirect(entries(n2_t, h * HALF, HALF)), root[t][:, cols], ALU.mult
                 )
-            nc.vector.scalar_tensor_tensor(z2_t[:, t, :], u[:], gb_t[:, t : t + 1], roots[t][:], ALU.mult, ALU.mult)
+
+        def z2_rows(t):
+            nc.vector.scalar_tensor_tensor(z2_t[:, t, :], u[t][:], gb_t[:, t : t + 1], root[t][:], ALU.mult, ALU.mult)
+
+        def a_out(t):
+            nc.vector.tensor_copy(a_sb[t][:], a_bank[t][:])
+            if t > 0:
+                nc.vector.tensor_tensor(sq[t][:, :N], a_bank[t][:], a_sb[t][:], ALU.mult)
+
+        member_sums(0, 0, mb[0])
+        member_sums(1, 0, mb[1])
+        a_out(1)
+        xb_w = pick_words(two_t, "w1w_d")
+        w2w_d = keep.tile([P, N], I32, name="w2w_d", align_bytes=64)
+        w2s_d = keep.tile([P, N], U8, name="w2s_d", align_bytes=64)
+        deal(w2w_d, w2w, 0, PACK)
+        deal(w2s_d, w2s, 0, PACK)
+        for t in range(3):
+            product(b_bank[t], w2w_d, w2s_d, xb_w, xb_s, t)
+        member_sums(0, 1, mb[2])
+        member_sums(1, 1, mb[3])
+        a_out(2)
+        product(b_bank[3], w2w_d, w2s_d, xb_w, xb_s, 3)
+        member_sums(0, 2, mb[0])
+        member_sums(1, 2, mb[1])
+        b_out(0)
+        b_out(1)
+        fetch_n3(0)
+        a_out(3)
+        den_sum(0)
+        fetch_n3(1)
+        den_root(0)
+        b_out(2)
+        den_sum(1)
+        member_sums(0, 3, g3[0])
+        fetch_n3(2)
+        den_root(1)
+        b_out(3)
+        member_sums(1, 3, g3[1])
+        fetch_n2(0)
+        den_sum(2)
+        fetch_n3(3)
+        roots_of_sums(0, r_t[0])
+        den_root(2)
+        z2_rows(0)
+        a_out(0)
+        fetch_n2(1)
+        den_sum(3)
+        roots_of_sums(1, r_t[1])
+        den_root(3)
+        member_sums(2, 0, den[0])
+        z2_rows(1)
+        z_chunk(0)
+        member_sums(2, 1, den[1])
+        fetch_n2(2)
+        z_weave(0)
+        z2_rows(2)
+        member_sums(2, 2, den[2])
+        member_sums(2, 3, den[3])
+        fetch_n2(3)
+        z_chunk(1)
+        z2_rows(3)
+        z_weave(1)
+        member_sums(3, 0, den[0])
+        roots_of_sums(2, r_t[2])
+        member_sums(3, 1, den[3])
+
         z2_il = keep.tile([P, N, PACK], BF16, name="z2_il", align_bytes=64)
         nc.vector.tensor_copy(z2_il[:], z2_t[:].rearrange("p k v -> p v k"))
         z2_w = keep.tile([P, N], U32, name="z2_w", align_bytes=64)
         z2_s = keep.tile([P, N], U8, name="z2_s", align_bytes=64)
         nc.vector.quantize_mx(out=z2_w[:].bitcast(FP8X4), scales=z2_s[:], in_=z2_il[:].rearrange("p v k -> p (v k)"))
+        z_chunk(2)
+        z_weave(2)
+        last_sums = keep.tile([P, 2, P], F32, name="last_sums")
 
-        member_sums(3, 0)
-        finish_z(2)
-        for t in range(1, PACK):
-            member_sums(3, t)
-        finish_z(3)
+        def fetch_and_add(t, buf, first, count):
+            nc.scalar.activation(
+                buf[:, first : first + count], sq[t][:].indirect(entries(n1_t, 3 * N + first, count)), ACT.Copy
+            )
+            nc.vector.tensor_reduce(
+                last_sums[:, t - 2, first // 4 : (first + count) // 4],
+                buf[:, first : first + count].rearrange("p (j e) -> p j e", e=4),
+                axis=mybir.AxisListType.X, op=ALU.add,
+            )
+
+        def root_in_place(t):
+            nc.scalar.activation(
+                r_t[3][:, t * P : (t + 1) * P], last_sums[:, t - 2, :], ACT.Abs_reciprocal_sqrt, bias=half[:]
+            )
+
+        fetch_and_add(2, den[0], 0, N)
+        roots_of_sums(3, r_t[3], range(2))
+        z_chunk(3, range(2))
+        root_in_place(2)
+        fetch_and_add(3, den[3], 0, HALF)
+        nc.vector.scalar_tensor_tensor(
+            z_c[1][:, 2, :], r_t[3][:, 2 * P : 3 * P], ga_t[:, 2:3], a_sb[2][:, 3 * P :], ALU.mult, ALU.mult
+        )
+        fetch_and_add(3, den[3], HALF, HALF)
+        z_weave(3, 3)
+        root_in_place(3)
+        nc.vector.scalar_tensor_tensor(
+            z_il[:, :, 96:, 3], r_t[3][:, 3 * P :].rearrange("p (m u) -> p u m", u=PACK), ga_t[:, 3:4],
+            a_sb[3][:, 3 * P :].rearrange("p (m u) -> p u m", u=PACK), ALU.mult, ALU.mult,
+        )
 
         z_w = keep.tile([P, N], U32, name="z_w", align_bytes=64)
         z_s = keep.tile([P, N], U8, name="z_s", align_bytes=64)
@@ -220,37 +311,77 @@ def tile_picked_kqgvarnorm2hopp_none_po_kernel(
             nc.vector.quantize_mx(
                 out=z_w[:, cols].bitcast(FP8X4), scales=z_s[:, cols], in_=z_il[:, t].rearrange("p m k -> p (m k)")
             )
+            product(s_bank[t], z_w, z_s, z2_w, z2_s, t)
 
         y = keep.tile([P, PACK, N], F32, name="y")
         out_rows = out_0.rearrange("(p t) v -> p t v", t=PACK)
-        for t in range(PACK):
-            acc = product(z_w, z_s, z2_w, z2_s, t)
-            s2 = ring.tile([P, N], F32, name="s2")
-            nc.scalar.activation(s2[:], acc[:], ACT.Copy, scale=0.125)
-            g4 = ring.tile([P, N], F32, name="g4")
+        s2, g4, st2, sg = rows("s2_"), rows("g4_"), rows("st2_"), rows("sg")
+
+        def s_out(t):
+            nc.scalar.activation(s2[t][:], s_bank[t][:], ACT.Copy, scale=0.125)
+
+        def fetch_n4(t, on_scalar):
             for h in range(2):
                 cols = slice(h * HALF, (h + 1) * HALF)
-                looked_up = s2[:].indirect(entries(n4_t, h * HALF, HALF))
-                if t == 1:
-                    nc.scalar.activation(g4[:, cols], looked_up, ACT.Copy)
+                looked_up = s2[t][:].indirect(entries(n4_t, h * HALF, HALF))
+                if on_scalar:
+                    nc.scalar.activation(g4[t][:, cols], looked_up, ACT.Copy)
                 else:
-                    nc.vector.tensor_copy(g4[:, cols], looked_up)
-            st2 = ring.tile([P, N], F32, name="st2")
-            nc.vector.scalar_tensor_tensor(st2[:], acc[:], 0.125, g4[:], ALU.mult, ALU.add)
-            sg = ring.tile([P, N], F32, name="sg")
+                    nc.vector.tensor_copy(g4[t][:, cols], looked_up)
+
+        def st_rows(t):
+            nc.vector.scalar_tensor_tensor(st2[t][:], s_bank[t][:], 0.125, g4[t][:], ALU.mult, ALU.add)
+
+        def fetch_n5(t):
             for h in range(2):
                 nc.scalar.activation(
-                    sg[:, h * HALF : (h + 1) * HALF], st2[:].indirect(entries(n5_t, h * HALF, HALF)), ACT.Sigmoid
+                    sg[t][:, h * HALF : (h + 1) * HALF], st2[t][:].indirect(entries(n5_t, h * HALF, HALF)), ACT.Sigmoid
                 )
-            nc.vector.scalar_tensor_tensor(y[:, t, :], sg[:], -0.5, st2[:], ALU.add, ALU.mult)
+
+        def y_rows(t, cols):
+            nc.vector.scalar_tensor_tensor(y[:, t, cols], sg[t][:, cols], -0.5, st2[t][:, cols], ALU.add, ALU.mult)
+
+        def y_store(t):
             nc.sync.dma_start(out_rows[:, t, :], y[:, t, :])
 
         y_il = keep.tile([P, N, PACK], BF16, name="y_il", align_bytes=64)
-        nc.vector.tensor_copy(y_il[:], y[:].rearrange("p t v -> p v t"))
         y_w = keep.tile([P, N], I32, name="y_w", align_bytes=64)
         y_s = keep.tile([P, N], U8, name="y_s", align_bytes=64)
-        nc.vector.quantize_mx(out=y_w[:].bitcast(FP8X4), scales=y_s[:], in_=y_il[:].rearrange("p v t -> p (v t)"))
-        nc.sync.dma_start(out_1[0].rearrange("p c r -> p (c r)").bitcast(I32), y_w[:])
+        words_out = out_1[0].rearrange("p c r -> p (c r)").bitcast(I32)
+
+        def y_weave(cols, copy):
+            copy(y_il[:, cols, :], y[:, :, cols].rearrange("p t v -> p v t"))
+
+        def y_quantise(cols):
+            nc.vector.quantize_mx(
+                out=y_w[:, cols].bitcast(FP8X4), scales=y_s[:, cols], in_=y_il[:, cols, :].rearrange("p v t -> p (v t)")
+            )
+            nc.sync.dma_start(words_out[:, cols], y_w[:, cols])
+
+        for t in range(PACK):
+            s_out(t)
+        fetch_n4(0, False)
+        st_rows(0)
+        fetch_n4(2, False)
+        fetch_n4(1, True)
+        fetch_n5(0)
+        st_rows(2)
+        st_rows(1)
+        fetch_n4(3, False)
+        fetch_n5(2)
+        st_rows(3)
+        fetch_n5(1)
+        fetch_n5(3)
+        for t in (0, 2, 1):
+            y_rows(t, whole)
+            y_store(t)
+        y_rows(3, left)
+        y_rows(3, right)
+        y_store(3)
+        y_weave(left, nc.scalar.copy)
+        y_weave(right, nc.vector.tensor_copy)
+        y_quantise(right)
+        y_quantise(left)
         for q in range(4):
             queue = nc.sync if q < 2 else nc.scalar
             queue.dma_start(out_2[0, 4 * q : 4 * q + 4, :].bitcast(I32), y_s[32 * q : 32 * q + 4, :].bitcast(I32))

@@ -88,6 +88,8 @@ def tile_picked_kqgvarnorm2hopp_none_po_kernel(
 
         half = keep.tile([P, 1], F32, name="half")
         nc.vector.memset(half[:], 0.5)
+        warm = keep.tile([P, 2], F32, name="warm")
+        nc.scalar.activation(warm[:, 0:1], half[:], ACT.Abs_reciprocal_sqrt, bias=half[:])
         sq = [keep.tile([P, N + SPARE], F32, name="sq%d" % t) for t in range(PACK)]
         for t in range(PACK):
             nc.vector.memset(sq[t][:, N:], 0.0)
@@ -299,6 +301,7 @@ def tile_picked_kqgvarnorm2hopp_none_po_kernel(
         fetch_and_add(3, den[3], HALF, HALF)
         z_weave(3, 3)
         root_in_place(3)
+        nc.scalar.activation(warm[:, 1:2], r_t[3][:, N - 1 : N], ACT.Sigmoid)
         nc.vector.scalar_tensor_tensor(
             z_il[:, :, 96:, 3], r_t[3][:, 3 * P :].rearrange("p (m u) -> p u m", u=PACK), ga_t[:, 3:4],
             a_sb[3][:, 3 * P :].rearrange("p (m u) -> p u m", u=PACK), ALU.mult, ALU.mult,

@@ -59,9 +59,9 @@ def tile_picked_kqgvarnorm2hopp_none_po_kernel(
         w1s = scale_tile(N, "w1s", nc.gpsimd)
         xs = scale_tile(T, "xs", nc.vector)
         w2s = scale_tile(N, "w2s", nc.vector)
-        offs_t = load_list(offs, "offs_t")
         xs_raw = keep.tile([P, T], U8, name="xs_raw", align_bytes=64)
         load_scales(xs_raw, x_scales, [nc.sync] * 4)
+        offs_t = load_list(offs, "offs_t")
         xw = keep.tile([P, T], I32, name="xw", align_bytes=64)
         load_words(xw, x_words)
         w1w = keep.tile([P, N], I32, name="w1w", align_bytes=64)
@@ -104,6 +104,11 @@ def tile_picked_kqgvarnorm2hopp_none_po_kernel(
             nc.vector.tensor_copy(tile[:], xw[:].bitcast(U32).indirect(lst[:]))
             return tile
 
+        def deal_words(src, first, last, name, engine):
+            tile = keep.tile([P, last - first, P], I32, name=name, align_bytes=64)
+            engine.tensor_copy(tile[:], src[:].rearrange("p (m t) -> p t m", t=PACK)[:, first:last, :])
+            return [tile[:, i, :] for i in range(last - first)]
+
         def deal(dealt, src, first, last, engine=nc.vector):
             engine.tensor_copy(
                 dealt[:].rearrange("p (t m) -> p t m", t=PACK)[:, first:last, :],
@@ -114,8 +119,12 @@ def tile_picked_kqgvarnorm2hopp_none_po_kernel(
 
         def product(acc, lhs_words, lhs_scales, rhs_words, rhs_scales, t):
             cols = slice(t * P, (t + 1) * P)
+            if isinstance(lhs_words, list):
+                lhs_words = lhs_words[t]
+            else:
+                lhs_words = lhs_words[:, cols]
             nc.tensor.matmul_mx(
-                out=acc[:], lhsT=lhs_words[:, cols].bitcast(FP8X4), lhsT_scale=lhs_scales[:, cols],
+                out=acc[:], lhsT=lhs_words.bitcast(FP8X4), lhsT_scale=lhs_scales[:, cols],
                 rhs=rhs_words[:].bitcast(FP8X4), rhs_scale=rhs_scales[:], start=True, stop=True,
             )
 
@@ -124,21 +133,26 @@ def tile_picked_kqgvarnorm2hopp_none_po_kernel(
 
         xa_s = pick_scales(offs_t, "xa_s")
         xa_w = pick_words(offs_t, "xa_w")
-        w1w_d = keep.tile([P, N], I32, name="w1w_d", align_bytes=64)
         w1s_d = keep.tile([P, N], U8, name="w1s_d", align_bytes=64)
         a_bank = bank[0:4]
-        deal(w1w_d, w1w, 0, 1)
+        w1w_d = deal_words(w1w, 0, 1, "w1_0", nc.vector)
         deal(w1s_d, w1s, 0, 1)
         product(a_bank[0], w1w_d, w1s_d, xa_w, xa_s, 0)
         nc.scalar.activation(sq[0][:, :N], a_bank[0][:], ACT.Square)
-        deal(w1w_d, w1w, 1, PACK)
+        w1w_d = w1w_d + deal_words(w1w, 1, 2, "w1_1", nc.vector) + deal_words(w1w, 2, 4, "w1_23", nc.vector)
         deal(w1s_d, w1s, 1, PACK)
         for t in range(1, PACK):
             product(a_bank[t], w1w_d, w1s_d, xa_w, xa_s, t)
         xb_s = pick_scales(two_t, "xb_s")
 
-        a_sb, b_sb, b_abs, g3, den, root, mb, r_t = (rows(n) for n in ("a", "b", "babs", "g3_", "den", "root", "mb", "rt"))
-        g3 = [g3[0], g3[1], den[0], den[1]]
+        def pairs(name):
+            return [keep.tile([P, 2 * N], F32, name="%s%d" % (name, t)) for t in range(PACK)]
+
+        g3, den, root, r_t = (rows(n) for n in ("g3_", "den", "root", "rt"))
+        ba, bm = pairs("ba"), pairs("bm")
+        b_sb, a_sb = [x[:, :N] for x in ba], [x[:, N:] for x in ba]
+        b_abs, mb = [x[:, :N] for x in bm], [x[:, N:] for x in bm]
+        g3 = [g3[0], mb[3], den[0], den[1]]
         b_bank = [bank[6], bank[7], bank[1], bank[2]]
         sum_bank = [bank[4], bank[5], bank[6], bank[7]]
         back_bank = [bank[3], bank[0], bank[4], bank[5]]
@@ -179,10 +193,7 @@ def tile_picked_kqgvarnorm2hopp_none_po_kernel(
             nc.vector.scalar_tensor_tensor(b_abs[t][:], b_bank[t][:], -1.0, b_sb[t][:], ALU.mult, ALU.max)
 
         def fetch_n3(t):
-            for h in range(2):
-                nc.scalar.activation(
-                    g3[t][:, h * HALF : (h + 1) * HALF], b_abs[t][:].indirect(entries(n3_t, h * HALF, HALF)), ACT.Copy
-                )
+            nc.scalar.activation(g3[t][:], bm[t][:].indirect(n3_t[:]), ACT.Copy)
 
         def den_sum(t):
             nc.vector.tensor_tensor(den[t][:], g3[t][:], b_abs[t][:], ALU.add)
@@ -194,11 +205,7 @@ def tile_picked_kqgvarnorm2hopp_none_po_kernel(
         z2_t = keep.tile([P, PACK, N], BF16, name="z2_t")
 
         def fetch_n2(t):
-            for h in range(2):
-                cols = slice(h * HALF, (h + 1) * HALF)
-                nc.vector.tensor_tensor(
-                    u[t][:, cols], b_sb[t][:].indirect(entries(n2_t, h * HALF, HALF)), root[t][:, cols], ALU.mult
-                )
+            nc.vector.tensor_tensor(u[t][:], ba[t][:].indirect(n2_t[:]), root[t][:], ALU.mult)
 
         def z2_rows(t):
             nc.vector.scalar_tensor_tensor(z2_t[:, t, :], u[t][:], gb_t[:, t : t + 1], root[t][:], ALU.mult, ALU.mult)
@@ -210,20 +217,20 @@ def tile_picked_kqgvarnorm2hopp_none_po_kernel(
 
         member_sums(0, 0, mb[0])
         member_sums(1, 0, mb[1])
-        a_out(1)
-        xb_w = pick_words(two_t, "w1w_d")
-        w2w_d = keep.tile([P, N], I32, name="w2w_d", align_bytes=64)
+        nc.vector.tensor_copy(a_sb[1][:], a_bank[1][:])
+        xb_w = pick_words(two_t, "w1_1")
+        nc.vector.tensor_tensor(sq[1][:, :N], a_bank[1][:], a_sb[1][:], ALU.mult)
         w2s_d = keep.tile([P, N], U8, name="w2s_d", align_bytes=64)
-        deal(w2w_d, w2w, 0, PACK)
-        deal(w2s_d, w2s, 0, PACK)
+        w2w_d = deal_words(w2w, 0, 1, "w2_0", nc.gpsimd) + deal_words(w2w, 1, 2, "w2_1", nc.gpsimd) + deal_words(w2w, 2, 4, "w2_23", nc.gpsimd)
+        deal(w2s_d, w2s, 0, PACK, nc.gpsimd)
         for t in range(3):
             product(b_bank[t], w2w_d, w2s_d, xb_w, xb_s, t)
-        member_sums(0, 1, mb[2])
-        member_sums(1, 1, mb[3])
+        member_sums(0, 1, keep.tile([P, N], F32, name="w2_0", align_bytes=64))
+        member_sums(1, 1, keep.tile([P, N], F32, name="w2_1", align_bytes=64))
         a_out(2)
         product(b_bank[3], w2w_d, w2s_d, xb_w, xb_s, 3)
-        member_sums(0, 2, mb[0])
-        member_sums(1, 2, mb[1])
+        member_sums(0, 2, mb[2])
+        member_sums(1, 2, keep.tile([P, N], F32, name="w2_23", align_bytes=64))
         b_out(0)
         b_out(1)
         fetch_n3(0)
@@ -238,13 +245,13 @@ def tile_picked_kqgvarnorm2hopp_none_po_kernel(
         den_root(1)
         b_out(3)
         member_sums(1, 3, g3[1])
+        a_out(0)
         fetch_n2(0)
         den_sum(2)
         fetch_n3(3)
         roots_of_sums(0, r_t[0])
         den_root(2)
         z2_rows(0)
-        a_out(0)
         fetch_n2(1)
         den_sum(3)
         roots_of_sums(1, r_t[1])
@@ -318,28 +325,30 @@ def tile_picked_kqgvarnorm2hopp_none_po_kernel(
 
         y = keep.tile([P, PACK, N], F32, name="y")
         out_rows = out_0.rearrange("(p t) v -> p t v", t=PACK)
-        s2, g4, st2, sg = rows("s2_"), rows("g4_"), rows("st2_"), rows("sg")
+        sg, stg = rows("sg"), pairs("stg")
+        s2 = b_sb
+        st2, g4 = [x[:, :N] for x in stg], [x[:, N:] for x in stg]
 
         def s_out(t):
-            nc.scalar.activation(s2[t][:], s_bank[t][:], ACT.Copy, scale=0.125)
+            if t == 0:
+                nc.vector.tensor_scalar(s2[t][:], s_bank[t][:], 0.125, None, ALU.mult)
+            else:
+                nc.scalar.activation(s2[t][:], s_bank[t][:], ACT.Copy, scale=0.125)
 
-        def fetch_n4(t, on_scalar):
-            for h in range(2):
-                cols = slice(h * HALF, (h + 1) * HALF)
-                looked_up = s2[t][:].indirect(entries(n4_t, h * HALF, HALF))
-                if on_scalar:
-                    nc.scalar.activation(g4[t][:, cols], looked_up, ACT.Copy)
-                else:
-                    nc.vector.tensor_copy(g4[t][:, cols], looked_up)
+        def fetch_n4(t, on_scalar, cols=whole):
+            looked_up = ba[t][:].indirect(entries(n4_t, cols.start, cols.stop - cols.start))
+            if on_scalar:
+                nc.scalar.activation(g4[t][:, cols], looked_up, ACT.Copy)
+            else:
+                nc.vector.tensor_copy(g4[t][:, cols], looked_up)
 
         def st_rows(t):
             nc.vector.scalar_tensor_tensor(st2[t][:], s_bank[t][:], 0.125, g4[t][:], ALU.mult, ALU.add)
 
-        def fetch_n5(t):
-            for h in range(2):
-                nc.scalar.activation(
-                    sg[t][:, h * HALF : (h + 1) * HALF], st2[t][:].indirect(entries(n5_t, h * HALF, HALF)), ACT.Sigmoid
-                )
+        def fetch_n5(t, cols=whole):
+            nc.scalar.activation(
+                sg[t][:, cols], stg[t][:].indirect(entries(n5_t, cols.start, cols.stop - cols.start)), ACT.Sigmoid
+            )
 
         def y_rows(t, cols):
             nc.vector.scalar_tensor_tensor(y[:, t, cols], sg[t][:, cols], -0.5, st2[t][:, cols], ALU.add, ALU.mult)
@@ -361,28 +370,35 @@ def tile_picked_kqgvarnorm2hopp_none_po_kernel(
             )
             nc.sync.dma_start(words_out[:, cols], y_w[:, cols])
 
-        for t in range(PACK):
+        for t in range(3):
             s_out(t)
         fetch_n4(0, False)
         st_rows(0)
         fetch_n4(2, False)
         fetch_n4(1, True)
+        s_out(3)
         fetch_n5(0)
         st_rows(2)
         st_rows(1)
-        fetch_n4(3, False)
+        fetch_n4(3, False, right)
+        fetch_n4(3, True, left)
         fetch_n5(2)
         st_rows(3)
         fetch_n5(1)
-        fetch_n5(3)
+        fetch_n5(3, left)
+        third, fourth = slice(HALF, HALF + P), slice(HALF + P, N)
+        fetch_n5(3, third)
+        fetch_n5(3, fourth)
         for t in (0, 2, 1):
             y_rows(t, whole)
             y_store(t)
         y_rows(3, left)
-        y_rows(3, right)
-        y_store(3)
+        y_rows(3, third)
         y_weave(left, nc.scalar.copy)
-        y_weave(right, nc.vector.tensor_copy)
+        y_weave(third, nc.vector.tensor_copy)
+        y_rows(3, fourth)
+        y_store(3)
+        y_weave(fourth, nc.vector.tensor_copy)
         y_quantise(right)
         y_quantise(left)
         for q in range(4):

@@ -14,12 +14,16 @@ ALU = mybir.AluOpType
 ACT = mybir.ActivationFunctionType
 
 P = 128
-PACK = 4
+TILES = 4
 N = 512
-T = 2048
-HALF = N // 2
-LIST_COL = 16
+TOKENS = 2048
+MEMBERS = 4
+QUADRANTS = 4
+LIST_COLUMN = 16
 SPARE = 16
+LAST = TILES - 1
+HALF = N // 2
+TWO_S = 0.125
 
 FLOPS = 3 * 2 * N * N * N
 
@@ -34,373 +38,387 @@ def tile_picked_kqgvarnorm2hopp_none_po_kernel(
         psum = ctx.enter_context(tc.psum_pool(name="psum", bufs=1))
         bank = [psum.tile([P, N], F32, name="bank%d" % i) for i in range(8)]
 
+        def block(i):
+            return slice(i * P, (i + 1) * P)
+
+        def row_tiles(name, count=TILES, width=N):
+            return [keep.tile([P, width], F32, name="%s%d" % (name, t)) for t in range(count)]
+
+        def entries(lst, cols):
+            return lst[:, cols.start // LIST_COLUMN : cols.stop // LIST_COLUMN]
+
         def load_list(src, name):
             tile = keep.tile(list(src.shape), U16, name=name)
             nc.sync.dma_start(tile[:], src)
             return tile
 
-        def load_words(tile, src):
+        def load_words(src, name):
+            tile = keep.tile([P, src.shape[2]], I32, name=name, align_bytes=64)
             nc.sync.dma_start(tile[:], src[0].rearrange("p c r -> p (c r)").bitcast(I32))
-
-        def scale_tile(width, name, clear):
-            tile = keep.tile([P, width], U8, name=name, align_bytes=64)
-            clear.memset(tile[:].bitcast(I32), 0)
             return tile
 
-        def load_scales(tile, src, queues):
-            for q in range(4):
-                queues[q].dma_start(
-                    tile[32 * q : 32 * q + 4, :].bitcast(I32), src[0, 4 * q : 4 * q + 4, :].bitcast(I32)
-                )
+        def zeroed_scales(width, name, engine):
+            tile = keep.tile([P, width], U8, name=name, align_bytes=64)
+            engine.memset(tile[:].bitcast(I32), 0)
+            return tile
 
-        def entries(lst, first, count):
-            return lst[:, first // LIST_COL : (first + count) // LIST_COL]
+        def scale_rows(tile, q):
+            return tile[32 * q : 32 * q + 4, :].bitcast(I32)
 
-        w1s = scale_tile(N, "w1s", nc.gpsimd)
-        xs = scale_tile(T, "xs", nc.vector)
-        w2s = scale_tile(N, "w2s", nc.vector)
-        xs_raw = keep.tile([P, T], U8, name="xs_raw", align_bytes=64)
-        load_scales(xs_raw, x_scales, [nc.sync] * 4)
+        def load_scales(tile, src):
+            for q in range(QUADRANTS):
+                nc.sync.dma_start(scale_rows(tile, q), src[0, 4 * q : 4 * q + 4, :].bitcast(I32))
+
+        def load_gains(src, name):
+            tile = keep.tile([P, TILES], F32, name=name)
+            nc.gpsimd.dma_start(tile[:], src.rearrange("(p t) o -> p (t o)", t=TILES))
+            return tile
+
+        w1_sc = zeroed_scales(N, "w1_sc", nc.gpsimd)
+        x_sc = zeroed_scales(TOKENS, "x_sc", nc.vector)
+        w2_sc = zeroed_scales(N, "w2_sc", nc.vector)
+        x_sc_landing = keep.tile([P, TOKENS], U8, name="x_sc_landing", align_bytes=64)
+        load_scales(x_sc_landing, x_scales)
         offs_t = load_list(offs, "offs_t")
-        xw = keep.tile([P, T], I32, name="xw", align_bytes=64)
-        load_words(xw, x_words)
-        w1w = keep.tile([P, N], I32, name="w1w", align_bytes=64)
-        load_words(w1w, w1_words)
-        load_scales(w1s, w1_scales, [nc.sync] * 4)
+        x_wd = load_words(x_words, "x_wd")
+        w1_wd = load_words(w1_words, "w1_wd")
+        load_scales(w1_sc, w1_scales)
         two_t = load_list(two, "two_t")
         n1_t = load_list(n1, "n1_t")
-        w2w = keep.tile([P, N], I32, name="w2w", align_bytes=64)
-        load_words(w2w, w2_words)
-        load_scales(w2s, w2_scales, [nc.sync] * 4)
+        w2_wd = load_words(w2_words, "w2_wd")
+        load_scales(w2_sc, w2_scales)
         n3_t = load_list(n3, "n3_t")
         n2_t = load_list(n2, "n2_t")
         n4_t = load_list(n4, "n4_t")
         n5_t = load_list(n5, "n5_t")
         ident = keep.tile([P, P], F32, name="ident")
         make_identity(nc, ident[:])
-        ga_t = keep.tile([P, PACK], F32, name="ga_t")
-        nc.gpsimd.dma_start(ga_t[:], ga.rearrange("(p t) o -> p (t o)", t=PACK))
-        gb_t = keep.tile([P, PACK], F32, name="gb_t")
-        nc.gpsimd.dma_start(gb_t[:], gb.rearrange("(p t) o -> p (t o)", t=PACK))
-        for q in range(4):
-            live = slice(32 * q, 32 * q + 4)
-            nc.vector.tensor_copy(xs[live, :].bitcast(I32), xs_raw[live, :].bitcast(I32))
+        ga_t = load_gains(ga, "ga_t")
+        gb_t = load_gains(gb, "gb_t")
+        for q in range(QUADRANTS):
+            nc.vector.tensor_copy(scale_rows(x_sc, q), scale_rows(x_sc_landing, q))
 
         half = keep.tile([P, 1], F32, name="half")
         nc.vector.memset(half[:], 0.5)
         warm = keep.tile([P, 2], F32, name="warm")
         nc.scalar.activation(warm[:, 0:1], half[:], ACT.Abs_reciprocal_sqrt, bias=half[:])
-        sq = [keep.tile([P, N + SPARE], F32, name="sq%d" % t) for t in range(PACK)]
-        for t in range(PACK):
-            nc.vector.memset(sq[t][:, N:], 0.0)
+        squares = row_tiles("squares", width=N + SPARE)
+        for t in range(TILES):
+            nc.vector.memset(squares[t][:, N:], 0.0)
 
         def pick_scales(lst, name):
             tile = keep.tile([P, N], U8, name=name, align_bytes=64)
-            nc.vector.tensor_copy(tile[:], xs[:].indirect(lst[:]))
+            nc.vector.tensor_copy(tile[:], x_sc[:].indirect(lst[:]))
             return tile
 
         def pick_words(lst, name):
             tile = keep.tile([P, N], U32, name=name, align_bytes=64)
-            nc.vector.tensor_copy(tile[:], xw[:].bitcast(U32).indirect(lst[:]))
+            nc.vector.tensor_copy(tile[:], x_wd[:].bitcast(U32).indirect(lst[:]))
             return tile
 
-        def deal_words(src, first, last, name, engine):
+        def by_slice(src, first, last):
+            return src[:].rearrange("p (m t) -> p t m", t=TILES)[:, first:last, :]
+
+        def deal_words(engine, src, first, last, name):
             tile = keep.tile([P, last - first, P], I32, name=name, align_bytes=64)
-            engine.tensor_copy(tile[:], src[:].rearrange("p (m t) -> p t m", t=PACK)[:, first:last, :])
+            engine.tensor_copy(tile[:], by_slice(src, first, last))
             return [tile[:, i, :] for i in range(last - first)]
 
-        def deal(dealt, src, first, last, engine=nc.vector):
+        def deal_scales(engine, dealt, src, first, last):
             engine.tensor_copy(
-                dealt[:].rearrange("p (t m) -> p t m", t=PACK)[:, first:last, :],
-                src[:].rearrange("p (m t) -> p t m", t=PACK)[:, first:last, :],
+                dealt[:].rearrange("p (t m) -> p t m", t=TILES)[:, first:last, :], by_slice(src, first, last)
             )
 
-        whole, left, right = slice(0, N), slice(0, HALF), slice(HALF, N)
-
-        def product(acc, lhs_words, lhs_scales, rhs_words, rhs_scales, t):
-            cols = slice(t * P, (t + 1) * P)
-            if isinstance(lhs_words, list):
-                lhs_words = lhs_words[t]
-            else:
-                lhs_words = lhs_words[:, cols]
+        def product(acc, lhs_words, lhs_scales, rhs_words, rhs_scales):
             nc.tensor.matmul_mx(
-                out=acc[:], lhsT=lhs_words.bitcast(FP8X4), lhsT_scale=lhs_scales[:, cols],
+                out=acc[:], lhsT=lhs_words.bitcast(FP8X4), lhsT_scale=lhs_scales,
                 rhs=rhs_words[:].bitcast(FP8X4), rhs_scale=rhs_scales[:], start=True, stop=True,
             )
 
-        def rows(name):
-            return [keep.tile([P, N], F32, name="%s%d" % (name, t)) for t in range(PACK)]
-
-        xa_s = pick_scales(offs_t, "xa_s")
-        xa_w = pick_words(offs_t, "xa_w")
-        w1s_d = keep.tile([P, N], U8, name="w1s_d", align_bytes=64)
         a_bank = bank[0:4]
-        w1w_d = deal_words(w1w, 0, 1, "w1_0", nc.vector)
-        deal(w1s_d, w1s, 0, 1)
-        product(a_bank[0], w1w_d, w1s_d, xa_w, xa_s, 0)
-        nc.scalar.activation(sq[0][:, :N], a_bank[0][:], ACT.Square)
-        w1w_d = w1w_d + deal_words(w1w, 1, 2, "w1_1", nc.vector) + deal_words(w1w, 2, 4, "w1_23", nc.vector)
-        deal(w1s_d, w1s, 1, PACK)
-        for t in range(1, PACK):
-            product(a_bank[t], w1w_d, w1s_d, xa_w, xa_s, t)
-        xb_s = pick_scales(two_t, "xb_s")
-
-        def pairs(name):
-            return [keep.tile([P, 2 * N], F32, name="%s%d" % (name, t)) for t in range(PACK)]
-
-        g3, den, root, r_t = (rows(n) for n in ("g3_", "den", "root", "rt"))
-        ba, bm = pairs("ba"), pairs("bm")
-        b_sb, a_sb = [x[:, :N] for x in ba], [x[:, N:] for x in ba]
-        b_abs, mb = [x[:, :N] for x in bm], [x[:, N:] for x in bm]
-        g3 = [g3[0], mb[3], den[0], den[1]]
         b_bank = [bank[6], bank[7], bank[1], bank[2]]
         sum_bank = [bank[4], bank[5], bank[6], bank[7]]
-        back_bank = [bank[3], bank[0], bank[4], bank[5]]
+        root_bank = [bank[3], bank[0], bank[4], bank[5]]
         s_bank = [bank[0], bank[3], bank[6], bank[4]]
 
+        xa_sc = pick_scales(offs_t, "xa_sc")
+        xa_wd = pick_words(offs_t, "xa_wd")
+        w1_sc_dealt = keep.tile([P, N], U8, name="w1_sc_dealt", align_bytes=64)
+        w1_dealt = deal_words(nc.vector, w1_wd, 0, 1, "w1_slice0")
+        deal_scales(nc.vector, w1_sc_dealt, w1_sc, 0, 1)
+        product(a_bank[0], w1_dealt[0], w1_sc_dealt[:, block(0)], xa_wd, xa_sc)
+        nc.scalar.activation(squares[0][:, :N], a_bank[0][:], ACT.Square)
+        w1_dealt = w1_dealt + deal_words(nc.vector, w1_wd, 1, 2, "w1_slice1_then_xb")
+        w1_dealt = w1_dealt + deal_words(nc.vector, w1_wd, 2, TILES, "w1_slices23")
+        deal_scales(nc.vector, w1_sc_dealt, w1_sc, 1, TILES)
+        for t in range(1, TILES):
+            product(a_bank[t], w1_dealt[t], w1_sc_dealt[:, block(t)], xa_wd, xa_sc)
+        xb_sc = pick_scales(two_t, "xb_sc")
+
+        work = row_tiles("work", TILES + 1)
+        den = work[1:]
+        den_root = row_tiles("den_root")
+        sum_root = row_tiles("sum_root")
+        b_and_a, abs_and_room = row_tiles("b_and_a", width=2 * N), row_tiles("abs_and_room", width=2 * N)
+        b_rows, a_rows = [x[:, :N] for x in b_and_a], [x[:, N:] for x in b_and_a]
+        b_abs, room = [x[:, :N] for x in abs_and_room], [x[:, N:] for x in abs_and_room]
+        abs_n3 = [work[0], room[LAST], den[0], den[1]]
+
+        def a_copy(t):
+            nc.vector.tensor_copy(a_rows[t][:], a_bank[t][:])
+
+        def a_square(t):
+            nc.vector.tensor_tensor(squares[t][:, :N], a_bank[t][:], a_rows[t][:], ALU.mult)
+
+        def fetch_members(c, t, buf, cols):
+            listed = slice(c * N + cols.start, c * N + cols.stop)
+            nc.scalar.activation(buf[:, cols], squares[t][:].indirect(entries(n1_t, listed)), ACT.Copy)
+
+        whole, left, right = slice(0, N), slice(0, HALF), slice(HALF, N)
+
         def member_sums(c, t, buf):
-            nc.scalar.activation(buf[:], sq[t][:].indirect(entries(n1_t, c * N, N)), ACT.Copy)
-            for e in range(4):
+            fetch_members(c, t, buf, whole)
+            for e in range(MEMBERS):
                 nc.tensor.matmul(
-                    sum_bank[c][:, t * P : (t + 1) * P], lhsT=buf[:, e:N:4], rhs=ident[:], is_transpose=True,
-                    start=(e == 0), stop=(e == 3),
+                    sum_bank[c][:, block(t)], lhsT=buf[:, e:N:MEMBERS], rhs=ident[:], is_transpose=True,
+                    start=(e == 0), stop=(e == MEMBERS - 1),
                 )
 
-        z_c = [keep.tile([P, PACK, P], BF16, name="z_c%d" % i) for i in range(2)]
-        z_il = keep.tile([P, PACK, P, PACK], BF16, name="z_il", align_bytes=64)
+        z_chunk = [keep.tile([P, TILES, P], BF16, name="z_chunk%d" % i) for i in range(2)]
+        z_woven = keep.tile([P, TILES, P, TILES], BF16, name="z_woven", align_bytes=64)
+        places = P // TILES
 
-        def roots_of_sums(c, buf, tiles=range(PACK)):
-            cols = slice(tiles[0] * P, (tiles[-1] + 1) * P)
-            nc.scalar.activation(buf[:, cols], sum_bank[c][:, cols], ACT.Abs_reciprocal_sqrt, bias=half[:])
-            for t in tiles:
-                nc.tensor.transpose(back_bank[c][:, t * P : (t + 1) * P], buf[:, t * P : (t + 1) * P], ident[:])
+        def roots_of_sums(c, tiles=TILES):
+            cols = slice(0, tiles * P)
+            nc.scalar.activation(sum_root[c][:, cols], sum_bank[c][:, cols], ACT.Abs_reciprocal_sqrt, bias=half[:])
+            for t in range(tiles):
+                nc.tensor.transpose(root_bank[c][:, block(t)], sum_root[c][:, block(t)], ident[:])
 
-        def z_chunk(c, tiles=range(PACK)):
-            for t in tiles:
-                nc.vector.scalar_tensor_tensor(
-                    z_c[c % 2][:, t, :], back_bank[c][:, t * P : (t + 1) * P], ga_t[:, t : t + 1],
-                    a_sb[t][:, c * P : (c + 1) * P], ALU.mult, ALU.mult,
-                )
+        def z_piece(out, root, t, a_piece):
+            nc.vector.scalar_tensor_tensor(out, root, ga_t[:, t : t + 1], a_piece, ALU.mult, ALU.mult)
 
-        def z_weave(c, tiles=PACK):
+        def z_pieces(c, tiles=TILES):
+            for t in range(tiles):
+                z_piece(z_chunk[c % 2][:, t, :], root_bank[c][:, block(t)], t, a_rows[t][:, block(c)])
+
+        def z_weave(c, tiles=TILES):
             nc.vector.tensor_copy(
-                z_il[:, :, 32 * c : 32 * (c + 1), :tiles],
-                z_c[c % 2][:, :tiles, :].rearrange("p k (m u) -> p u m k", u=PACK),
+                z_woven[:, :, places * c : places * (c + 1), :tiles],
+                z_chunk[c % 2][:, :tiles, :].rearrange("p k (m u) -> p u m k", u=TILES),
             )
 
         def b_out(t):
-            nc.vector.tensor_copy(b_sb[t][:], b_bank[t][:])
-            nc.vector.scalar_tensor_tensor(b_abs[t][:], b_bank[t][:], -1.0, b_sb[t][:], ALU.mult, ALU.max)
+            nc.vector.tensor_copy(b_rows[t][:], b_bank[t][:])
+            nc.vector.scalar_tensor_tensor(b_abs[t][:], b_bank[t][:], -1.0, b_rows[t][:], ALU.mult, ALU.max)
 
         def fetch_n3(t):
-            nc.scalar.activation(g3[t][:], bm[t][:].indirect(n3_t[:]), ACT.Copy)
+            nc.scalar.activation(abs_n3[t][:], abs_and_room[t][:].indirect(n3_t[:]), ACT.Copy)
 
         def den_sum(t):
-            nc.vector.tensor_tensor(den[t][:], g3[t][:], b_abs[t][:], ALU.add)
+            nc.vector.tensor_tensor(den[t][:], abs_n3[t][:], b_abs[t][:], ALU.add)
 
-        def den_root(t):
-            nc.scalar.activation(root[t][:], den[t][:], ACT.Abs_reciprocal_sqrt, bias=half[:])
+        def den_inverse_root(t):
+            nc.scalar.activation(den_root[t][:], den[t][:], ACT.Abs_reciprocal_sqrt, bias=half[:])
 
-        u = rows("u")
-        z2_t = keep.tile([P, PACK, N], BF16, name="z2_t")
+        b_n2 = row_tiles("b_n2")
+        z2_rows = keep.tile([P, TILES, N], BF16, name="z2_rows")
 
         def fetch_n2(t):
-            nc.vector.tensor_tensor(u[t][:], ba[t][:].indirect(n2_t[:]), root[t][:], ALU.mult)
+            nc.vector.tensor_tensor(b_n2[t][:], b_and_a[t][:].indirect(n2_t[:]), den_root[t][:], ALU.mult)
 
-        def z2_rows(t):
-            nc.vector.scalar_tensor_tensor(z2_t[:, t, :], u[t][:], gb_t[:, t : t + 1], root[t][:], ALU.mult, ALU.mult)
+        def z2_row(t):
+            nc.vector.scalar_tensor_tensor(
+                z2_rows[:, t, :], b_n2[t][:], gb_t[:, t : t + 1], den_root[t][:], ALU.mult, ALU.mult
+            )
 
-        def a_out(t):
-            nc.vector.tensor_copy(a_sb[t][:], a_bank[t][:])
-            if t > 0:
-                nc.vector.tensor_tensor(sq[t][:, :N], a_bank[t][:], a_sb[t][:], ALU.mult)
+        member_sums(0, 0, room[0])
+        member_sums(1, 0, room[1])
+        a_copy(1)
+        xb_wd = pick_words(two_t, "w1_slice1_then_xb")
+        a_square(1)
+        w2_sc_dealt = keep.tile([P, N], U8, name="w2_sc_dealt", align_bytes=64)
+        w2_dealt = deal_words(nc.gpsimd, w2_wd, 0, 1, "w2_slice0_then_members")
+        w2_dealt = w2_dealt + deal_words(nc.gpsimd, w2_wd, 1, TILES, "w2_slices123")
+        deal_scales(nc.gpsimd, w2_sc_dealt, w2_sc, 0, TILES)
+        for t in range(LAST):
+            product(b_bank[t], w2_dealt[t], w2_sc_dealt[:, block(t)], xb_wd, xb_sc)
+        member_sums(0, 1, keep.tile([P, N], F32, name="w2_slice0_then_members", align_bytes=64))
+        member_sums(1, 1, room[2])
+        a_copy(2)
+        a_square(2)
+        product(b_bank[LAST], w2_dealt[LAST], w2_sc_dealt[:, block(LAST)], xb_wd, xb_sc)
+        member_sums(0, 2, room[0])
+        member_sums(1, 2, room[1])
 
-        member_sums(0, 0, mb[0])
-        member_sums(1, 0, mb[1])
-        nc.vector.tensor_copy(a_sb[1][:], a_bank[1][:])
-        xb_w = pick_words(two_t, "w1_1")
-        nc.vector.tensor_tensor(sq[1][:, :N], a_bank[1][:], a_sb[1][:], ALU.mult)
-        w2s_d = keep.tile([P, N], U8, name="w2s_d", align_bytes=64)
-        w2w_d = deal_words(w2w, 0, 1, "w2_0", nc.gpsimd) + deal_words(w2w, 1, 2, "w2_1", nc.gpsimd) + deal_words(w2w, 2, 4, "w2_23", nc.gpsimd)
-        deal(w2s_d, w2s, 0, PACK, nc.gpsimd)
-        for t in range(3):
-            product(b_bank[t], w2w_d, w2s_d, xb_w, xb_s, t)
-        member_sums(0, 1, keep.tile([P, N], F32, name="w2_0", align_bytes=64))
-        member_sums(1, 1, keep.tile([P, N], F32, name="w2_1", align_bytes=64))
-        a_out(2)
-        product(b_bank[3], w2w_d, w2s_d, xb_w, xb_s, 3)
-        member_sums(0, 2, mb[2])
-        member_sums(1, 2, keep.tile([P, N], F32, name="w2_23", align_bytes=64))
         b_out(0)
         b_out(1)
         fetch_n3(0)
-        a_out(3)
+        a_copy(3)
+        a_square(3)
         den_sum(0)
         fetch_n3(1)
-        den_root(0)
+        den_inverse_root(0)
         b_out(2)
         den_sum(1)
-        member_sums(0, 3, g3[0])
+        member_sums(0, 3, abs_n3[0])
         fetch_n3(2)
-        den_root(1)
+        den_inverse_root(1)
         b_out(3)
-        member_sums(1, 3, g3[1])
-        a_out(0)
+        member_sums(1, 3, abs_n3[1])
+
+        a_copy(0)
         fetch_n2(0)
         den_sum(2)
         fetch_n3(3)
-        roots_of_sums(0, r_t[0])
-        den_root(2)
-        z2_rows(0)
+        roots_of_sums(0)
+        den_inverse_root(2)
+        z2_row(0)
         fetch_n2(1)
         den_sum(3)
-        roots_of_sums(1, r_t[1])
-        den_root(3)
+        roots_of_sums(1)
+        den_inverse_root(3)
         member_sums(2, 0, den[0])
-        z2_rows(1)
-        z_chunk(0)
+        z2_row(1)
+
+        z_pieces(0)
         member_sums(2, 1, den[1])
         fetch_n2(2)
         z_weave(0)
-        z2_rows(2)
+        z2_row(2)
         member_sums(2, 2, den[2])
         member_sums(2, 3, den[3])
         fetch_n2(3)
-        z_chunk(1)
-        z2_rows(3)
+        z_pieces(1)
+        z2_row(3)
         z_weave(1)
         member_sums(3, 0, den[0])
-        roots_of_sums(2, r_t[2])
+        roots_of_sums(2)
         member_sums(3, 1, den[3])
 
-        z2_il = keep.tile([P, N, PACK], BF16, name="z2_il", align_bytes=64)
-        nc.vector.tensor_copy(z2_il[:], z2_t[:].rearrange("p k v -> p v k"))
-        z2_w = keep.tile([P, N], U32, name="z2_w", align_bytes=64)
-        z2_s = keep.tile([P, N], U8, name="z2_s", align_bytes=64)
-        nc.vector.quantize_mx(out=z2_w[:].bitcast(FP8X4), scales=z2_s[:], in_=z2_il[:].rearrange("p v k -> p (v k)"))
-        z_chunk(2)
+        z2_woven = keep.tile([P, N, TILES], BF16, name="z2_woven", align_bytes=64)
+        nc.vector.tensor_copy(z2_woven[:], z2_rows[:].rearrange("p k v -> p v k"))
+        z2_wd = keep.tile([P, N], U32, name="z2_wd", align_bytes=64)
+        z2_sc = keep.tile([P, N], U8, name="z2_sc", align_bytes=64)
+        nc.vector.quantize_mx(
+            out=z2_wd[:].bitcast(FP8X4), scales=z2_sc[:], in_=z2_woven[:].rearrange("p v k -> p (v k)")
+        )
+        z_pieces(2)
         z_weave(2)
-        last_sums = keep.tile([P, 2, P], F32, name="last_sums")
 
-        def fetch_and_add(t, buf, first, count):
-            nc.scalar.activation(
-                buf[:, first : first + count], sq[t][:].indirect(entries(n1_t, 3 * N + first, count)), ACT.Copy
-            )
+        on_tensor = 2
+        plain_sums = keep.tile([P, TILES - on_tensor, P], F32, name="plain_sums")
+        plain_root = keep.tile([P, TILES - on_tensor, P], F32, name="plain_root")
+
+        def fetch_and_add(t, buf, cols):
+            fetch_members(LAST, t, buf, cols)
             nc.vector.tensor_reduce(
-                last_sums[:, t - 2, first // 4 : (first + count) // 4],
-                buf[:, first : first + count].rearrange("p (j e) -> p j e", e=4),
+                plain_sums[:, t - on_tensor, cols.start // MEMBERS : cols.stop // MEMBERS],
+                buf[:, cols].rearrange("p (j e) -> p j e", e=MEMBERS),
                 axis=mybir.AxisListType.X, op=ALU.add,
             )
 
-        def root_in_place(t):
-            nc.scalar.activation(
-                r_t[3][:, t * P : (t + 1) * P], last_sums[:, t - 2, :], ACT.Abs_reciprocal_sqrt, bias=half[:]
-            )
+        def plain_inverse_root(t):
+            i = t - on_tensor
+            nc.scalar.activation(plain_root[:, i, :], plain_sums[:, i, :], ACT.Abs_reciprocal_sqrt, bias=half[:])
+            return plain_root[:, i, :]
 
-        fetch_and_add(2, den[0], 0, N)
-        roots_of_sums(3, r_t[3], range(2))
-        z_chunk(3, range(2))
-        root_in_place(2)
-        fetch_and_add(3, den[3], 0, HALF)
-        nc.vector.scalar_tensor_tensor(
-            z_c[1][:, 2, :], r_t[3][:, 2 * P : 3 * P], ga_t[:, 2:3], a_sb[2][:, 3 * P :], ALU.mult, ALU.mult
-        )
-        fetch_and_add(3, den[3], HALF, HALF)
-        z_weave(3, 3)
-        root_in_place(3)
-        nc.scalar.activation(warm[:, 1:2], r_t[3][:, N - 1 : N], ACT.Sigmoid)
-        nc.vector.scalar_tensor_tensor(
-            z_il[:, :, 96:, 3], r_t[3][:, 3 * P :].rearrange("p (m u) -> p u m", u=PACK), ga_t[:, 3:4],
-            a_sb[3][:, 3 * P :].rearrange("p (m u) -> p u m", u=PACK), ALU.mult, ALU.mult,
+        fetch_and_add(2, den[0], whole)
+        roots_of_sums(LAST, on_tensor)
+        z_pieces(LAST, on_tensor)
+        root_2 = plain_inverse_root(2)
+        fetch_and_add(3, den[3], slice(0, N - P))
+        z_piece(z_chunk[LAST % 2][:, 2, :], root_2, 2, a_rows[2][:, block(LAST)])
+        fetch_and_add(3, den[3], block(LAST))
+        z_weave(LAST, LAST)
+        root_3 = plain_inverse_root(3)
+        nc.scalar.activation(warm[:, 1:2], root_3[:, P - 1 : P], ACT.Sigmoid)
+        z_piece(
+            z_woven[:, :, places * LAST :, LAST], root_3.rearrange("p (m u) -> p u m", u=TILES), LAST,
+            a_rows[LAST][:, block(LAST)].rearrange("p (m u) -> p u m", u=TILES),
         )
 
-        z_w = keep.tile([P, N], U32, name="z_w", align_bytes=64)
-        z_s = keep.tile([P, N], U8, name="z_s", align_bytes=64)
-        for t in range(PACK):
-            cols = slice(t * P, (t + 1) * P)
+        z_wd = keep.tile([P, N], U32, name="z_wd", align_bytes=64)
+        z_sc = keep.tile([P, N], U8, name="z_sc", align_bytes=64)
+        for u in range(TILES):
             nc.vector.quantize_mx(
-                out=z_w[:, cols].bitcast(FP8X4), scales=z_s[:, cols], in_=z_il[:, t].rearrange("p m k -> p (m k)")
+                out=z_wd[:, block(u)].bitcast(FP8X4), scales=z_sc[:, block(u)],
+                in_=z_woven[:, u].rearrange("p m k -> p (m k)"),
             )
-            product(s_bank[t], z_w, z_s, z2_w, z2_s, t)
+            product(s_bank[u], z_wd[:, block(u)], z_sc[:, block(u)], z2_wd, z2_sc)
 
-        y = keep.tile([P, PACK, N], F32, name="y")
-        out_rows = out_0.rearrange("(p t) v -> p t v", t=PACK)
-        sg, stg = rows("sg"), pairs("stg")
-        s2 = b_sb
-        st2, g4 = [x[:, :N] for x in stg], [x[:, N:] for x in stg]
+        y = keep.tile([P, TILES, N], F32, name="y")
+        out_rows = out_0.rearrange("(p t) v -> p t v", t=TILES)
+        gate, st_and_n4 = row_tiles("gate"), row_tiles("st_and_n4", width=2 * N)
+        s_window = b_and_a
+        two_st, two_s_n4 = [x[:, :N] for x in st_and_n4], [x[:, N:] for x in st_and_n4]
 
         def s_out(t):
-            if t == 0:
-                nc.vector.tensor_scalar(s2[t][:], s_bank[t][:], 0.125, None, ALU.mult)
-            else:
-                nc.scalar.activation(s2[t][:], s_bank[t][:], ACT.Copy, scale=0.125)
+            nc.scalar.activation(s_window[t][:, :N], s_bank[t][:], ACT.Copy, scale=TWO_S)
 
-        def fetch_n4(t, on_scalar, cols=whole):
-            looked_up = ba[t][:].indirect(entries(n4_t, cols.start, cols.stop - cols.start))
-            if on_scalar:
-                nc.scalar.activation(g4[t][:, cols], looked_up, ACT.Copy)
-            else:
-                nc.vector.tensor_copy(g4[t][:, cols], looked_up)
+        def fetch_n4_vector(t, cols=whole):
+            nc.vector.tensor_copy(two_s_n4[t][:, cols], s_window[t][:].indirect(entries(n4_t, cols)))
 
-        def st_rows(t):
-            nc.vector.scalar_tensor_tensor(st2[t][:], s_bank[t][:], 0.125, g4[t][:], ALU.mult, ALU.add)
+        def fetch_n4_scalar(t, cols=whole):
+            nc.scalar.activation(two_s_n4[t][:, cols], s_window[t][:].indirect(entries(n4_t, cols)), ACT.Copy)
+
+        def st_row(t):
+            nc.vector.scalar_tensor_tensor(two_st[t][:], s_bank[t][:], TWO_S, two_s_n4[t][:], ALU.mult, ALU.add)
 
         def fetch_n5(t, cols=whole):
-            nc.scalar.activation(
-                sg[t][:, cols], stg[t][:].indirect(entries(n5_t, cols.start, cols.stop - cols.start)), ACT.Sigmoid
-            )
+            nc.scalar.activation(gate[t][:, cols], st_and_n4[t][:].indirect(entries(n5_t, cols)), ACT.Sigmoid)
 
-        def y_rows(t, cols):
-            nc.vector.scalar_tensor_tensor(y[:, t, cols], sg[t][:, cols], -0.5, st2[t][:, cols], ALU.add, ALU.mult)
+        def y_row(t, cols=whole):
+            nc.vector.scalar_tensor_tensor(y[:, t, cols], gate[t][:, cols], -0.5, two_st[t][:, cols], ALU.add, ALU.mult)
 
         def y_store(t):
             nc.sync.dma_start(out_rows[:, t, :], y[:, t, :])
 
-        y_il = keep.tile([P, N, PACK], BF16, name="y_il", align_bytes=64)
-        y_w = keep.tile([P, N], I32, name="y_w", align_bytes=64)
-        y_s = keep.tile([P, N], U8, name="y_s", align_bytes=64)
+        y_woven = keep.tile([P, N, TILES], BF16, name="y_woven", align_bytes=64)
+        y_wd = keep.tile([P, N], I32, name="y_wd", align_bytes=64)
+        y_sc = keep.tile([P, N], U8, name="y_sc", align_bytes=64)
         words_out = out_1[0].rearrange("p c r -> p (c r)").bitcast(I32)
 
-        def y_weave(cols, copy):
-            copy(y_il[:, cols, :], y[:, :, cols].rearrange("p t v -> p v t"))
+        def y_weave(copy, cols):
+            copy(y_woven[:, cols, :], y[:, :, cols].rearrange("p t v -> p v t"))
 
         def y_quantise(cols):
             nc.vector.quantize_mx(
-                out=y_w[:, cols].bitcast(FP8X4), scales=y_s[:, cols], in_=y_il[:, cols, :].rearrange("p v t -> p (v t)")
+                out=y_wd[:, cols].bitcast(FP8X4), scales=y_sc[:, cols],
+                in_=y_woven[:, cols, :].rearrange("p v t -> p (v t)"),
             )
-            nc.sync.dma_start(words_out[:, cols], y_w[:, cols])
+            nc.sync.dma_start(words_out[:, cols], y_wd[:, cols])
 
-        for t in range(3):
-            s_out(t)
-        fetch_n4(0, False)
-        st_rows(0)
-        fetch_n4(2, False)
-        fetch_n4(1, True)
+        nc.vector.tensor_scalar(s_window[0][:, :N], s_bank[0][:], TWO_S, None, ALU.mult)
+        s_out(1)
+        s_out(2)
+        fetch_n4_vector(0)
+        st_row(0)
+        fetch_n4_vector(2)
+        fetch_n4_scalar(1)
         s_out(3)
         fetch_n5(0)
-        st_rows(2)
-        st_rows(1)
-        fetch_n4(3, False, right)
-        fetch_n4(3, True, left)
+        st_row(2)
+        st_row(1)
+        fetch_n4_vector(3, right)
+        fetch_n4_scalar(3, left)
         fetch_n5(2)
-        st_rows(3)
+        st_row(3)
         fetch_n5(1)
-        fetch_n5(3, left)
-        third, fourth = slice(HALF, HALF + P), slice(HALF + P, N)
-        fetch_n5(3, third)
-        fetch_n5(3, fourth)
+        third, fourth = block(2), block(3)
+        for cols in (left, third, fourth):
+            fetch_n5(LAST, cols)
         for t in (0, 2, 1):
-            y_rows(t, whole)
+            y_row(t)
             y_store(t)
-        y_rows(3, left)
-        y_rows(3, third)
-        y_weave(left, nc.scalar.copy)
-        y_weave(third, nc.vector.tensor_copy)
-        y_rows(3, fourth)
-        y_store(3)
-        y_weave(fourth, nc.vector.tensor_copy)
+        y_row(LAST, left)
+        y_row(LAST, third)
+        y_weave(nc.scalar.copy, left)
+        y_weave(nc.vector.tensor_copy, third)
+        y_row(LAST, fourth)
+        y_store(LAST)
+        y_weave(nc.vector.tensor_copy, fourth)
         y_quantise(right)
         y_quantise(left)
-        for q in range(4):
-            queue = nc.sync if q < 2 else nc.scalar
-            queue.dma_start(out_2[0, 4 * q : 4 * q + 4, :].bitcast(I32), y_s[32 * q : 32 * q + 4, :].bitcast(I32))
+        for q in range(QUADRANTS):
+            queue = nc.sync if q < QUADRANTS // 2 else nc.scalar
+            queue.dma_start(out_2[0, 4 * q : 4 * q + 4, :].bitcast(I32), scale_rows(y_sc, q))

from contextlib import ExitStack

import concourse.mybir as mybir
from concourse.masks import make_identity

F32 = mybir.dt.float32
BF16 = mybir.dt.bfloat16
I32 = mybir.dt.int32
U32 = mybir.dt.uint32
U16 = mybir.dt.uint16
U8 = mybir.dt.uint8
FP8X4 = mybir.dt.float8_e4m3fn_x4
ALU = mybir.AluOpType
ACT = mybir.ActivationFunctionType

P = 128
TILES = 4
N = 512
TOKENS = 2048
MEMBERS = 4
QUADRANTS = 4
LIST_COLUMN = 16
SPARE = 16
LAST = TILES - 1
HALF = N // 2
TWO_S = 0.125

FLOPS = 3 * 2 * N * N * N


def tile_picked_kqgvarnorm2hopp_none_po_kernel(
    tc, x_words, x_scales, w1_words, w1_scales, w2_words, w2_scales, ga, gb,
    offs, two, n1, n2, n3, n4, n5, out_0, out_1, out_2,
):
    nc = tc.nc
    with ExitStack() as ctx:
        keep = ctx.enter_context(tc.tile_pool(name="keep", bufs=1))
        psum = ctx.enter_context(tc.psum_pool(name="psum", bufs=1))
        bank = [psum.tile([P, N], F32, name="bank%d" % i) for i in range(8)]

        def block(i):
            return slice(i * P, (i + 1) * P)

        def row_tiles(name, count=TILES, width=N):
            return [keep.tile([P, width], F32, name="%s%d" % (name, t)) for t in range(count)]

        def entries(lst, cols):
            return lst[:, cols.start // LIST_COLUMN : cols.stop // LIST_COLUMN]

        def load_list(src, name):
            tile = keep.tile(list(src.shape), U16, name=name)
            nc.sync.dma_start(tile[:], src)
            return tile

        def load_words(src, name):
            tile = keep.tile([P, src.shape[2]], I32, name=name, align_bytes=64)
            nc.sync.dma_start(tile[:], src[0].rearrange("p c r -> p (c r)").bitcast(I32))
            return tile

        def zeroed_scales(width, name, engine):
            tile = keep.tile([P, width], U8, name=name, align_bytes=64)
            engine.memset(tile[:].bitcast(I32), 0)
            return tile

        def scale_rows(tile, q):
            return tile[32 * q : 32 * q + 4, :].bitcast(I32)

        def load_scales(tile, src):
            for q in range(QUADRANTS):
                nc.sync.dma_start(scale_rows(tile, q), src[0, 4 * q : 4 * q + 4, :].bitcast(I32))

        def load_gains(src, name):
            tile = keep.tile([P, TILES], F32, name=name)
            nc.gpsimd.dma_start(tile[:], src.rearrange("(p t) o -> p (t o)", t=TILES))
            return tile

        w1_sc = zeroed_scales(N, "w1_sc", nc.gpsimd)
        x_sc = zeroed_scales(TOKENS, "x_sc", nc.vector)
        w2_sc = zeroed_scales(N, "w2_sc", nc.vector)
        x_sc_landing = keep.tile([P, TOKENS], U8, name="x_sc_landing", align_bytes=64)
        load_scales(x_sc_landing, x_scales)
        offs_t = load_list(offs, "offs_t")
        x_wd = load_words(x_words, "x_wd")
        w1_wd = load_words(w1_words, "w1_wd")
        load_scales(w1_sc, w1_scales)
        two_t = load_list(two, "two_t")
        n1_t = load_list(n1, "n1_t")
        w2_wd = load_words(w2_words, "w2_wd")
        load_scales(w2_sc, w2_scales)
        n3_t = load_list(n3, "n3_t")
        n2_t = load_list(n2, "n2_t")
        n4_t = load_list(n4, "n4_t")
        n5_t = load_list(n5, "n5_t")
        ident = keep.tile([P, P], F32, name="ident")
        make_identity(nc, ident[:])
        ga_t = load_gains(ga, "ga_t")
        gb_t = load_gains(gb, "gb_t")
        for q in range(QUADRANTS):
            nc.vector.tensor_copy(scale_rows(x_sc, q), scale_rows(x_sc_landing, q))

        half = keep.tile([P, 1], F32, name="half")
        nc.vector.memset(half[:], 0.5)
        warm = keep.tile([P, 2], F32, name="warm")
        nc.scalar.activation(warm[:, 0:1], half[:], ACT.Abs_reciprocal_sqrt, bias=half[:])
        squares = row_tiles("squares", width=N + SPARE)
        for t in range(TILES):
            nc.vector.memset(squares[t][:, N:], 0.0)

        def pick_scales(lst, name):
            tile = keep.tile([P, N], U8, name=name, align_bytes=64)
            nc.vector.tensor_copy(tile[:], x_sc[:].indirect(lst[:]))
            return tile

        def pick_words(lst, name):
            tile = keep.tile([P, N], U32, name=name, align_bytes=64)
            nc.vector.tensor_copy(tile[:], x_wd[:].bitcast(U32).indirect(lst[:]))
            return tile

        def by_slice(src, first, last):
            return src[:].rearrange("p (m t) -> p t m", t=TILES)[:, first:last, :]

        def deal_words(engine, src, first, last, name):
            tile = keep.tile([P, last - first, P], I32, name=name, align_bytes=64)
            engine.tensor_copy(tile[:], by_slice(src, first, last))
            return [tile[:, i, :] for i in range(last - first)]

        def deal_scales(engine, dealt, src, first, last):
            engine.tensor_copy(
                dealt[:].rearrange("p (t m) -> p t m", t=TILES)[:, first:last, :], by_slice(src, first, last)
            )

        def product(acc, lhs_words, lhs_scales, rhs_words, rhs_scales):
            nc.tensor.matmul_mx(
                out=acc[:], lhsT=lhs_words.bitcast(FP8X4), lhsT_scale=lhs_scales,
                rhs=rhs_words[:].bitcast(FP8X4), rhs_scale=rhs_scales[:], start=True, stop=True,
            )

        a_bank = bank[0:4]
        b_bank = [bank[6], bank[7], bank[1], bank[2]]
        sum_bank = [bank[4], bank[5], bank[6], bank[7]]
        root_bank = [bank[3], bank[0], bank[4], bank[5]]
        s_bank = [bank[0], bank[3], bank[6], bank[4]]

        xa_sc = pick_scales(offs_t, "xa_sc")
        xa_wd = pick_words(offs_t, "xa_wd")
        w1_sc_dealt = keep.tile([P, N], U8, name="w1_sc_dealt", align_bytes=64)
        w1_dealt = deal_words(nc.vector, w1_wd, 0, 1, "w1_slice0")
        deal_scales(nc.vector, w1_sc_dealt, w1_sc, 0, 1)
        product(a_bank[0], w1_dealt[0], w1_sc_dealt[:, block(0)], xa_wd, xa_sc)
        nc.scalar.activation(squares[0][:, :N], a_bank[0][:], ACT.Square)
        w1_dealt = w1_dealt + deal_words(nc.vector, w1_wd, 1, 2, "w1_slice1_then_xb")
        w1_dealt = w1_dealt + deal_words(nc.vector, w1_wd, 2, TILES, "w1_slices23")
        deal_scales(nc.vector, w1_sc_dealt, w1_sc, 1, TILES)
        for t in range(1, TILES):
            product(a_bank[t], w1_dealt[t], w1_sc_dealt[:, block(t)], xa_wd, xa_sc)
        xb_sc = pick_scales(two_t, "xb_sc")

        work = row_tiles("work", TILES + 1)
        den = work[1:]
        den_root = row_tiles("den_root")
        sum_root = row_tiles("sum_root")
        b_and_a, abs_and_room = row_tiles("b_and_a", width=2 * N), row_tiles("abs_and_room", width=2 * N)
        b_rows, a_rows = [x[:, :N] for x in b_and_a], [x[:, N:] for x in b_and_a]
        b_abs, room = [x[:, :N] for x in abs_and_room], [x[:, N:] for x in abs_and_room]
        abs_n3 = [work[0], room[LAST], den[0], den[1]]

        def a_copy(t):
            nc.vector.tensor_copy(a_rows[t][:], a_bank[t][:])

        def a_square(t):
            nc.vector.tensor_tensor(squares[t][:, :N], a_bank[t][:], a_rows[t][:], ALU.mult)

        def fetch_members(c, t, buf, cols):
            listed = slice(c * N + cols.start, c * N + cols.stop)
            nc.scalar.activation(buf[:, cols], squares[t][:].indirect(entries(n1_t, listed)), ACT.Copy)

        whole, left, right = slice(0, N), slice(0, HALF), slice(HALF, N)

        def member_sums(c, t, buf):
            fetch_members(c, t, buf, whole)
            for e in range(MEMBERS):
                nc.tensor.matmul(
                    sum_bank[c][:, block(t)], lhsT=buf[:, e:N:MEMBERS], rhs=ident[:], is_transpose=True,
                    start=(e == 0), stop=(e == MEMBERS - 1),
                )

        z_chunk = [keep.tile([P, TILES, P], BF16, name="z_chunk%d" % i) for i in range(2)]
        z_woven = keep.tile([P, TILES, P, TILES], BF16, name="z_woven", align_bytes=64)
        places = P // TILES

        def roots_of_sums(c, tiles=TILES):
            cols = slice(0, tiles * P)
            nc.scalar.activation(sum_root[c][:, cols], sum_bank[c][:, cols], ACT.Abs_reciprocal_sqrt, bias=half[:])
            for t in range(tiles):
                nc.tensor.transpose(root_bank[c][:, block(t)], sum_root[c][:, block(t)], ident[:])

        def z_piece(out, root, t, a_piece):
            nc.vector.scalar_tensor_tensor(out, root, ga_t[:, t : t + 1], a_piece, ALU.mult, ALU.mult)

        def z_pieces(c, tiles=TILES):
            for t in range(tiles):
                z_piece(z_chunk[c % 2][:, t, :], root_bank[c][:, block(t)], t, a_rows[t][:, block(c)])

        def z_weave(c, tiles=TILES):
            nc.vector.tensor_copy(
                z_woven[:, :, places * c : places * (c + 1), :tiles],
                z_chunk[c % 2][:, :tiles, :].rearrange("p k (m u) -> p u m k", u=TILES),
            )

        def b_out(t):
            nc.vector.tensor_copy(b_rows[t][:], b_bank[t][:])
            nc.vector.scalar_tensor_tensor(b_abs[t][:], b_bank[t][:], -1.0, b_rows[t][:], ALU.mult, ALU.max)

        def fetch_n3(t):
            nc.scalar.activation(abs_n3[t][:], abs_and_room[t][:].indirect(n3_t[:]), ACT.Copy)

        def den_sum(t):
            nc.vector.tensor_tensor(den[t][:], abs_n3[t][:], b_abs[t][:], ALU.add)

        def den_inverse_root(t):
            nc.scalar.activation(den_root[t][:], den[t][:], ACT.Abs_reciprocal_sqrt, bias=half[:])

        b_n2 = row_tiles("b_n2")
        z2_rows = keep.tile([P, TILES, N], BF16, name="z2_rows")

        def fetch_n2(t):
            nc.vector.tensor_tensor(b_n2[t][:], b_and_a[t][:].indirect(n2_t[:]), den_root[t][:], ALU.mult)

        def z2_row(t):
            nc.vector.scalar_tensor_tensor(
                z2_rows[:, t, :], b_n2[t][:], gb_t[:, t : t + 1], den_root[t][:], ALU.mult, ALU.mult
            )

        member_sums(0, 0, room[0])
        member_sums(1, 0, room[1])
        a_copy(1)
        xb_wd = pick_words(two_t, "w1_slice1_then_xb")
        a_square(1)
        w2_sc_dealt = keep.tile([P, N], U8, name="w2_sc_dealt", align_bytes=64)
        w2_dealt = deal_words(nc.gpsimd, w2_wd, 0, 1, "w2_slice0_then_members")
        w2_dealt = w2_dealt + deal_words(nc.gpsimd, w2_wd, 1, TILES, "w2_slices123")
        deal_scales(nc.gpsimd, w2_sc_dealt, w2_sc, 0, TILES)
        for t in range(LAST):
            product(b_bank[t], w2_dealt[t], w2_sc_dealt[:, block(t)], xb_wd, xb_sc)
        member_sums(0, 1, keep.tile([P, N], F32, name="w2_slice0_then_members", align_bytes=64))
        member_sums(1, 1, room[2])
        a_copy(2)
        a_square(2)
        product(b_bank[LAST], w2_dealt[LAST], w2_sc_dealt[:, block(LAST)], xb_wd, xb_sc)
        member_sums(0, 2, room[0])
        member_sums(1, 2, room[1])

        b_out(0)
        b_out(1)
        fetch_n3(0)
        a_copy(3)
        a_square(3)
        den_sum(0)
        fetch_n3(1)
        den_inverse_root(0)
        b_out(2)
        den_sum(1)
        member_sums(0, 3, abs_n3[0])
        fetch_n3(2)
        den_inverse_root(1)
        b_out(3)
        member_sums(1, 3, abs_n3[1])

        a_copy(0)
        fetch_n2(0)
        den_sum(2)
        fetch_n3(3)
        roots_of_sums(0)
        den_inverse_root(2)
        z2_row(0)
        fetch_n2(1)
        den_sum(3)
        roots_of_sums(1)
        den_inverse_root(3)
        member_sums(2, 0, den[0])
        z2_row(1)

        z_pieces(0)
        member_sums(2, 1, den[1])
        fetch_n2(2)
        z_weave(0)
        z2_row(2)
        member_sums(2, 2, den[2])
        member_sums(2, 3, den[3])
        fetch_n2(3)
        z_pieces(1)
        z2_row(3)
        z_weave(1)
        member_sums(3, 0, den[0])
        roots_of_sums(2)
        member_sums(3, 1, den[3])

        z2_woven = keep.tile([P, N, TILES], BF16, name="z2_woven", align_bytes=64)
        nc.vector.tensor_copy(z2_woven[:], z2_rows[:].rearrange("p k v -> p v k"))
        z2_wd = keep.tile([P, N], U32, name="z2_wd", align_bytes=64)
        z2_sc = keep.tile([P, N], U8, name="z2_sc", align_bytes=64)
        nc.vector.quantize_mx(
            out=z2_wd[:].bitcast(FP8X4), scales=z2_sc[:], in_=z2_woven[:].rearrange("p v k -> p (v k)")
        )
        z_pieces(2)
        z_weave(2)

        on_tensor = 2
        plain_sums = keep.tile([P, TILES - on_tensor, P], F32, name="plain_sums")
        plain_root = keep.tile([P, TILES - on_tensor, P], F32, name="plain_root")

        def fetch_and_add(t, buf, cols):
            fetch_members(LAST, t, buf, cols)
            nc.vector.tensor_reduce(
                plain_sums[:, t - on_tensor, cols.start // MEMBERS : cols.stop // MEMBERS],
                buf[:, cols].rearrange("p (j e) -> p j e", e=MEMBERS),
                axis=mybir.AxisListType.X, op=ALU.add,
            )

        def plain_inverse_root(t):
            i = t - on_tensor
            nc.scalar.activation(plain_root[:, i, :], plain_sums[:, i, :], ACT.Abs_reciprocal_sqrt, bias=half[:])
            return plain_root[:, i, :]

        fetch_and_add(2, den[0], whole)
        roots_of_sums(LAST, on_tensor)
        z_pieces(LAST, on_tensor)
        root_2 = plain_inverse_root(2)
        fetch_and_add(3, den[3], slice(0, N - P))
        z_piece(z_chunk[LAST % 2][:, 2, :], root_2, 2, a_rows[2][:, block(LAST)])
        fetch_and_add(3, den[3], block(LAST))
        z_weave(LAST, LAST)
        root_3 = plain_inverse_root(3)
        nc.scalar.activation(warm[:, 1:2], root_3[:, P - 1 : P], ACT.Sigmoid)
        z_piece(
            z_woven[:, :, places * LAST :, LAST], root_3.rearrange("p (m u) -> p u m", u=TILES), LAST,
            a_rows[LAST][:, block(LAST)].rearrange("p (m u) -> p u m", u=TILES),
        )

        z_wd = keep.tile([P, N], U32, name="z_wd", align_bytes=64)
        z_sc = keep.tile([P, N], U8, name="z_sc", align_bytes=64)
        for u in range(TILES):
            nc.vector.quantize_mx(
                out=z_wd[:, block(u)].bitcast(FP8X4), scales=z_sc[:, block(u)],
                in_=z_woven[:, u].rearrange("p m k -> p (m k)"),
            )
            product(s_bank[u], z_wd[:, block(u)], z_sc[:, block(u)], z2_wd, z2_sc)

        y = keep.tile([P, TILES, N], F32, name="y")
        out_rows = out_0.rearrange("(p t) v -> p t v", t=TILES)
        gate, st_and_n4 = row_tiles("gate"), row_tiles("st_and_n4", width=2 * N)
        s_window = b_and_a
        two_st, two_s_n4 = [x[:, :N] for x in st_and_n4], [x[:, N:] for x in st_and_n4]

        def s_out(t):
            nc.scalar.activation(s_window[t][:, :N], s_bank[t][:], ACT.Copy, scale=TWO_S)

        def fetch_n4_vector(t, cols=whole):
            nc.vector.tensor_copy(two_s_n4[t][:, cols], s_window[t][:].indirect(entries(n4_t, cols)))

        def fetch_n4_scalar(t, cols=whole):
            nc.scalar.activation(two_s_n4[t][:, cols], s_window[t][:].indirect(entries(n4_t, cols)), ACT.Copy)

        def st_row(t):
            nc.vector.scalar_tensor_tensor(two_st[t][:], s_bank[t][:], TWO_S, two_s_n4[t][:], ALU.mult, ALU.add)

        def fetch_n5(t, cols=whole):
            nc.scalar.activation(gate[t][:, cols], st_and_n4[t][:].indirect(entries(n5_t, cols)), ACT.Sigmoid)

        def y_row(t, cols=whole):
            nc.vector.scalar_tensor_tensor(y[:, t, cols], gate[t][:, cols], -0.5, two_st[t][:, cols], ALU.add, ALU.mult)

        def y_store(t):
            nc.sync.dma_start(out_rows[:, t, :], y[:, t, :])

        y_woven = keep.tile([P, N, TILES], BF16, name="y_woven", align_bytes=64)
        y_wd = keep.tile([P, N], I32, name="y_wd", align_bytes=64)
        y_sc = keep.tile([P, N], U8, name="y_sc", align_bytes=64)
        words_out = out_1[0].rearrange("p c r -> p (c r)").bitcast(I32)

        def y_weave(copy, cols):
            copy(y_woven[:, cols, :], y[:, :, cols].rearrange("p t v -> p v t"))

        def y_quantise(cols):
            nc.vector.quantize_mx(
                out=y_wd[:, cols].bitcast(FP8X4), scales=y_sc[:, cols],
                in_=y_woven[:, cols, :].rearrange("p v t -> p (v t)"),
            )
            nc.sync.dma_start(words_out[:, cols], y_wd[:, cols])

        nc.vector.tensor_scalar(s_window[0][:, :N], s_bank[0][:], TWO_S, None, ALU.mult)
        s_out(1)
        s_out(2)
        fetch_n4_vector(0)
        st_row(0)
        fetch_n4_vector(2)
        fetch_n4_scalar(1)
        s_out(3)
        fetch_n5(0)
        st_row(2)
        st_row(1)
        fetch_n4_vector(3, right)
        fetch_n4_scalar(3, left)
        fetch_n5(2)
        st_row(3)
        fetch_n5(1)
        third, fourth = block(2), block(3)
        for cols in (left, third, fourth):
            fetch_n5(LAST, cols)
        for t in (0, 2, 1):
            y_row(t)
            y_store(t)
        y_row(LAST, left)
        y_row(LAST, third)
        y_weave(nc.scalar.copy, left)
        y_weave(nc.vector.tensor_copy, third)
        y_row(LAST, fourth)
        y_store(LAST)
        y_weave(nc.vector.tensor_copy, fourth)
        y_quantise(right)
        y_quantise(left)
        for q in range(QUADRANTS):
            queue = nc.sync if q < QUADRANTS // 2 else nc.scalar
            queue.dma_start(out_2[0, 4 * q : 4 * q + 4, :].bitcast(I32), scale_rows(y_sc, q))
